import numpy as np
import ml_dtypes


def mxq(x, axis, fmt="e4m3"):
    dtype, down = {"e4m3": (ml_dtypes.float8_e4m3fn, 7), "e5m2": (ml_dtypes.float8_e5m2, 14)}[fmt]
    v = np.moveaxis(np.asarray(x, np.float32).astype(ml_dtypes.bfloat16).astype(np.float64), axis, -1)
    blocks = v.reshape(v.shape[:-1] + (-1, 32))
    amax = np.abs(blocks).max(-1, keepdims=True)
    byte = np.maximum(np.where(amax > 0, np.frexp(amax)[1] - 1 + 127, 0) - down, 1)
    scale = np.exp2(byte - 127.0)
    codes = (blocks / scale).astype(np.float32).astype(dtype).astype(np.float64)
    return np.moveaxis((codes * scale).reshape(v.shape), -1, axis)


WIDE = False


def mx_kscale(k):
    if not WIDE:
        return np.ones(k)
    levels = np.array([10, -10, 5, -5, 0])
    if k % 512:
        return np.exp2(np.random.permutation(np.resize(levels, k // 32))).repeat(32)
    a = np.empty((k // 512, 16))
    for p in range(k // 512):
        a[p, :8] = np.random.permutation(np.resize(levels, 8))
        for g in range(8):
            far = levels[np.abs(levels - a[p, g]) >= 10]
            a[p, g + 8] = far[np.random.randint(len(far))]
    return np.exp2(a.ravel()).repeat(32)


BF16 = ml_dtypes.bfloat16


def bf(x):
    return np.asarray(x, np.float32).astype(BF16)


def f64(x):
    return np.asarray(x).astype(np.float64)

def planes(Y):
    n, m = Y.shape
    b = f64(bf(Y)).reshape(n // 32, 32, m)
    amax = np.abs(b).max(1)
    byte = np.clip(np.where(amax > 0, np.frexp(amax)[1] - 1 + 127 - 7, 1), 1, 254)
    codes = (b * np.exp2(127.0 - byte)[:, None, :]).reshape(n, m).astype(np.float32).astype(ml_dtypes.float8_e4m3fn).view(np.uint8)
    words = codes.reshape(n // 512, 128, 4, m).transpose(0, 1, 3, 2)
    return np.ascontiguousarray(words), np.ascontiguousarray(byte.astype(np.uint8).reshape(n // 512, 16, m))


C, T, D, J = 2, 1024, 1024, 256


def complex_product(xr, xi, vr, vi):
    re = (xr @ vr) - (xi @ vi)
    im = (xr @ vi) + (xi @ vr)
    return re, im


def setup_inputs():
    s, u = mx_kscale(D), mx_kscale(T)
    return {"y": bf(np.random.standard_normal((C, T, D)) * s[None, None, :] * u[None, :, None]),
            "w": bf(np.random.standard_normal((C, D, J)) * 0.8 / np.sqrt(C * D)),
            "q": bf((1.0 + 0.1 * np.random.standard_normal(T)) / u),
            "a": bf((1.0 + 0.1 * np.random.standard_normal(D)) / s),
            "r": bf(np.random.uniform(0.5, 1.5, J))}


def core(y, w, q, a, r):
    y, w, q, a, r = f64(y), f64(w), f64(q), f64(a), f64(r)
    yr, yi = y[0], y[1]
    a_col = a[:, None]
    q_col = q[:, None]
    root_t = np.sqrt(y.shape[1])

    vr = mxq(a_col * w[0], 0, "e4m3")
    vi = mxq(a_col * w[1], 0, "e4m3")

    pr, pi = complex_product(mxq(yr, 1, "e4m3"), mxq(yi, 1, "e4m3"), vr, vi)
    zr = q_col * pr
    zi = q_col * pi

    m = zr * zr + zi * zi - r[None, :]

    er = mxq(q_col * m * zr / root_t, 0, "e4m3")
    ei = mxq(q_col * m * zi / root_t, 0, "e4m3")

    yr_t = mxq(yr.T, 1, "e4m3")
    yi_t = mxq(yi.T, 1, "e4m3")
    gr = a_col * ((yr_t @ er) + (yi_t @ ei))
    gi = a_col * ((yr_t @ ei) - (yi_t @ er))

    return np.stack([gr, gi], axis=0)


def reference(y, w, q, a, r):
    R_out = core(y, w, q, a, r)
    words, scales = planes(np.moveaxis(R_out, 1, 0).reshape(1024, -1))
    return R_out, words, scales

@@ -1,0 +1,404 @@
+from contextlib import ExitStack
+
+import concourse.mybir as mybir
+from concourse.masks import make_identity
+
+F32 = mybir.dt.float32
+BF16 = mybir.dt.bfloat16
+U32 = mybir.dt.uint32
+I32 = mybir.dt.int32
+U8 = mybir.dt.uint8
+FP8X4 = mybir.dt.float8_e4m3fn_x4
+ACT = mybir.ActivationFunctionType
+ALU = mybir.AluOpType
+
+P = 128
+C, T, D, J = 2, 1024, 1024, 256
+FLOPS = 8 * 2 * T * D * J
+
+
+def tile_godardconstantmodulusgradient_x1_kernel(tc, y, w, q, a, r, out, words, scales):
+    nc = tc.nc
+    with ExitStack() as ctx:
+        keep = ctx.enter_context(tc.tile_pool(name="keep", bufs=1))
+        stage = ctx.enter_context(tc.tile_pool(name="stage", bufs=4))
+        psum = ctx.enter_context(tc.psum_pool(name="psum", bufs=1))
+        ctx.enter_context(tc.manual_schedule())
+
+        def kt(name, shape, dt):
+            return keep.tile(shape, dt, name=name, align_bytes=64)
+
+        a_bf = kt("a_bf", [P, 2, 4], BF16)
+        q_bf = kt("q_bf", [P, 2, 4], BF16)
+        r_bf = kt("r_bf", [P, J], BF16)
+        nc.scalar.dma_start(out=a_bf[:], in_=a.rearrange("(g p j) -> p g j", p=P, j=4))
+        nc.scalar.dma_start(out=q_bf[:], in_=q.rearrange("(g p j) -> p g j", p=P, j=4))
+        nc.scalar.dma_start(out=r_bf[:], in_=r.partition_broadcast(P))
+        w_raw = {}
+        for G in (0, 1):
+            w_raw[G] = kt("w_raw%d" % G, [P, 2, 4, J], BF16)
+            for c in (0, 1):
+                nc.sync.dma_start(
+                    out=w_raw[G][:, c],
+                    in_=w[c, 512 * G : 512 * G + 512, :].rearrange("(p j) n -> p j n", j=4),
+                )
+        y_raw = {}
+        for g in (0, 1):
+            for c in (0, 1):
+                y_raw[c, g] = kt("y_raw%d%d" % (c, g), [P, 4, D], BF16)
+                src = y[c, 512 * g : 512 * g + 512, :].rearrange("(p j) d -> p j d", j=4)
+                for j0 in (0, 2):
+                    nc.sync.dma_start(out=y_raw[c, g][:, j0 : j0 + 2], in_=src[:, j0 : j0 + 2])
+
+        ident = kt("ident", [P, P], F32)
+        make_identity(nc, ident[:])
+
+        q2 = kt("q2", [P, 8], F32)
+        s_col = kt("s_col", [P, 8], F32)
+        k_col = kt("k_col", [P, 8], F32)
+        a_col = kt("a_col", [P, 8], F32)
+        qv = q_bf[:].rearrange("p g j -> p (g j)")
+        nc.vector.tensor_tensor(out=q2[:], in0=qv, in1=qv, op=ALU.mult)
+        nc.vector.tensor_copy(out=a_col[:], in_=a_bf[:].rearrange("p g j -> p (g j)"))
+        nc.vector.tensor_scalar(out=k_col[:], in0=q2[:], scalar1=2.0**-5, scalar2=None, op0=ALU.mult)
+        nc.vector.tensor_scalar(out=s_col[:], in0=q2[:], scalar1=2.0**-2.5, scalar2=None, op0=ALU.mult)
+
+        rr = kt("rr", [P, 2, 2, 4, 128], F32)
+
+        def r_scaled(g):
+            for j in range(4):
+                nc.scalar.activation(
+                    out=rr[:, g, :, j, :],
+                    in_=r_bf[:].rearrange("p (h n) -> p h n", h=2),
+                    func=ACT.Copy,
+                    scale=k_col[:, 4 * g + j : 4 * g + j + 1],
+                )
+
+        v_bf, v_codes, v_scales = {}, {}, {}
+        for G in (0, 1):
+            v_bf[G] = kt("v_bf%d" % G, [P, 3, J, 4], BF16)
+            v_codes[G] = kt("v_codes%d" % G, [P, 3 * J], U32)
+            v_scales[G] = kt("v_scales%d" % G, [P, 3 * J], U8)
+
+        def v_mult(G, c):
+            nc.vector.tensor_tensor(
+                out=v_bf[G][:, c],
+                in0=w_raw[G][:, c].rearrange("p j n -> p n j"),
+                in1=a_bf[:, G, :].unsqueeze(1).to_broadcast([P, J, 4]),
+                op=ALU.mult,
+            )
+
+        def v_neg(G):
+            vi = v_bf[G][:, 1].rearrange("p n j -> p (n j)")
+            vn = v_bf[G][:, 2].rearrange("p n j -> p (n j)")
+            if G == 0:
+                nc.scalar.activation(out=vn, in_=vi, func=ACT.Copy, scale=-1.0)
+            else:
+                nc.vector.tensor_scalar(out=vn, in0=vi, scalar1=-1.0, scalar2=None, op0=ALU.mult)
+
+        def v_quant(G, lo, n):
+            nc.vector.quantize_mx(
+                out=v_codes[G][:, lo * J : (lo + n) * J].bitcast(FP8X4),
+                scales=v_scales[G][:, lo * J : (lo + n) * J],
+                in_=v_bf[G][:, lo : lo + n].rearrange("p s n j -> p (s n j)"),
+            )
+
+        x_codes, x_scales, yt = {}, {}, {}
+        for c in (0, 1):
+            for g in (0, 1):
+                x_codes[c, g] = kt("x_codes%d%d" % (c, g), [P, 4, 2, P], U32)
+                x_scales[c, g] = kt("x_scales%d%d" % (c, g), [P, 4, 2, P], U8)
+
+        bank_of_t = [0]
+
+        def turn(c, g, j):
+            if j % 2 == 0:
+                yt[c, g] = stage.tile([P, 2, 2, P, 2], F32, name="yt", align_bytes=64)
+            b = bank_of_t[0] % 4
+            bank_of_t[0] += 1
+            tp = psum.tile([P, 2, 2, P], F32, name="tp", tag="b%d" % b)
+            wordsv = y_raw[c, g][:, j, :].bitcast(F32)
+            for G in (0, 1):
+                for u in (0, 1):
+                    nc.tensor.transpose(tp[:, G, u, :], wordsv[:, 256 * G + u : 256 * (G + 1) : 2], ident[:])
+            nc.scalar.copy(out=yt[c, g][:, j % 2], in_=tp[:].rearrange("p g u r -> p g r u"))
+
+        def x_quant(c, g, h):
+            nc.vector.quantize_mx(
+                out=x_codes[c, g][:, 2 * h : 2 * h + 2].rearrange("p j g r -> p (j g r)").bitcast(FP8X4),
+                scales=x_scales[c, g][:, 2 * h : 2 * h + 2].rearrange("p j g r -> p (j g r)"),
+                in_=yt[c, g][:].rearrange("p j g r u -> p (j g r u)").bitcast(BF16),
+            )
+
+        t_codes, t_scales, ti = {}, {}, {}
+        for c in (0, 1):
+            for g in (0, 1):
+                t_codes[c, g] = kt("t_codes%d%d" % (c, g), [P, D], U32)
+                t_scales[c, g] = kt("t_scales%d%d" % (c, g), [P, D], U8)
+
+        def t_weave(c, g, G, eng):
+            t = stage.tile([P, 4, P, 4], BF16, name="ti", align_bytes=64)
+            ti[c, g, G] = t
+            src = y_raw[c, g][:, :, 512 * G : 512 * G + 512].rearrange("p j (m t) -> p t m j", t=4)
+            if eng == "S":
+                nc.scalar.copy(out=t[:], in_=src)
+            else:
+                nc.vector.tensor_copy(out=t[:], in_=src)
+
+        def t_quant(c, g, G):
+            nc.vector.quantize_mx(
+                out=t_codes[c, g][:, 512 * G : 512 * G + 512].bitcast(FP8X4),
+                scales=t_scales[c, g][:, 512 * G : 512 * G + 512],
+                in_=ti[c, g, G][:].rearrange("p t m j -> p (t m j)"),
+            )
+
+        z = {}
+        sq, dev = {}, {}
+        e_bf, e_codes, e_scales = {}, {}, {}
+        for g in (0, 1):
+            e_bf[g] = kt("e_bf%d" % g, [P, 3, J, 4], BF16)
+            e_codes[g] = kt("e_codes%d" % g, [P, 3 * J], U32)
+            e_scales[g] = kt("e_scales%d" % g, [P, 3 * J], U8)
+
+        def stage1(g, h, x):
+            b = (4 if g == 0 else 0) + 2 * h + x
+            zt = psum.tile([P, 4, P], F32, name="z", tag="b%d" % b)
+            z[g, h, x] = zt
+            slots = (0, 2) if x == 0 else (1, 0)
+            for j in range(4):
+                n = 0
+                for c in (0, 1):
+                    lo = slots[c] * J + 128 * h
+                    for G in (0, 1):
+                        nc.tensor.matmul_mx(
+                            out=zt[:, j, :],
+                            lhsT=x_codes[c, g][:, j, G, :].bitcast(FP8X4),
+                            lhsT_scale=x_scales[c, g][:, j, G, :],
+                            rhs=v_codes[G][:, lo : lo + 128].bitcast(FP8X4),
+                            rhs_scale=v_scales[G][:, lo : lo + 128],
+                            start=(n == 0),
+                            stop=(n == 3),
+                        )
+                        n += 1
+
+        def squares(g, h, x):
+            if x == 0:
+                sq[g, h] = stage.tile([P, 2, 4, P], F32, name="sq", align_bytes=64, bufs=2)
+            for j in range(4):
+                nc.scalar.activation(
+                    out=sq[g, h][:, x, j, :],
+                    in_=z[g, h, x][:, j, :],
+                    func=ACT.Square,
+                    scale=s_col[:, 4 * g + j : 4 * g + j + 1],
+                )
+
+        def dev1(g, h):
+            u = stage.tile([P, 4, P], F32, name="u", align_bytes=64, bufs=2)
+            dev[g, h, 0] = u
+            nc.vector.tensor_tensor(out=u[:], in0=sq[g, h][:, 0], in1=rr[:, g, h], op=ALU.subtract)
+
+        def dev2(g, h):
+            m = stage.tile([P, 4, P], F32, name="m", align_bytes=64, bufs=2)
+            dev[g, h, 1] = m
+            nc.vector.tensor_tensor(out=m[:], in0=dev[g, h, 0][:], in1=sq[g, h][:, 1], op=ALU.add)
+
+        def err(g, h, x):
+            nc.vector.tensor_tensor(
+                out=e_bf[g][:, x, 128 * h : 128 * h + 128, :],
+                in0=z[g, h, x][:].rearrange("p j n -> p n j"),
+                in1=dev[g, h, 1][:].rearrange("p j n -> p n j"),
+                op=ALU.mult,
+            )
+
+        def err_neg(g, h):
+            nc.vector.tensor_scalar(
+                out=e_bf[g][:, 2, 128 * h : 128 * h + 128, :].rearrange("p n j -> p (n j)"),
+                in0=e_bf[g][:, 0, 128 * h : 128 * h + 128, :].rearrange("p n j -> p (n j)"),
+                scalar1=-1.0,
+                scalar2=None,
+                op0=ALU.mult,
+            )
+
+        def err_quant(g, h):
+            for x in (0, 1, 2):
+                lo = x * J + 128 * h
+                nc.vector.quantize_mx(
+                    out=e_codes[g][:, lo : lo + 128].bitcast(FP8X4),
+                    scales=e_scales[g][:, lo : lo + 128],
+                    in_=e_bf[g][:, x, 128 * h : 128 * h + 128, :].rearrange("p n j -> p (n j)"),
+                )
+
+        acc, res, ob, o_codes, o_scales = {}, {}, {}, {}, {}
+        for G in (0, 1):
+            res[G] = kt("res%d" % G, [P, 2, 4, J], F32)
+            ob[G] = kt("ob%d" % G, [P, 2 * J, 4], BF16)
+            o_codes[G] = kt("o_codes%d" % G, [P, 2 * J], U32)
+            o_scales[G] = kt("o_scales%d" % G, [P, 2 * J], U8)
+
+        def stage2(G, t, g):
+            if g == 0:
+                acc[G, t] = psum.tile([P, 2 * J], F32, name="acc", tag="b%d" % ((4 if G == 0 else 0) + t))
+            lo = 512 * G + 128 * t
+            for c in (0, 1):
+                nc.tensor.matmul_mx(
+                    out=acc[G, t][:],
+                    lhsT=t_codes[c, g][:, lo : lo + 128].bitcast(FP8X4),
+                    lhsT_scale=t_scales[c, g][:, lo : lo + 128],
+                    rhs=e_codes[g][:, c * J : c * J + 512].bitcast(FP8X4),
+                    rhs_scale=e_scales[g][:, c * J : c * J + 512],
+                    start=(g == 0 and c == 0),
+                    stop=(g == 1 and c == 1),
+                )
+
+        def leave(G, t):
+            nc.scalar.activation(
+                out=res[G][:, :, t, :],
+                in_=acc[G, t][:].rearrange("p (c n) -> p c n", c=2),
+                func=ACT.Copy,
+                scale=a_col[:, 4 * G + t : 4 * G + t + 1],
+            )
+
+        def out_weave(G, c):
+            nc.vector.tensor_copy(
+                out=ob[G][:, c * J : (c + 1) * J, :], in_=res[G][:, c].rearrange("p t n -> p n t")
+            )
+
+        def out_quant(G, c):
+            nc.vector.quantize_mx(
+                out=o_codes[G][:, c * J : (c + 1) * J].bitcast(FP8X4),
+                scales=o_scales[G][:, c * J : (c + 1) * J],
+                in_=ob[G][:, c * J : (c + 1) * J, :].rearrange("p n t -> p (n t)"),
+            )
+
+        def store_out(G):
+            for c in (0, 1):
+                nc.sync.dma_start(
+                    out=out[c, 512 * G : 512 * G + 512, :].rearrange("(p t) n -> p t n", t=4), in_=res[G][:, c]
+                )
+
+        def store_planes(G):
+            nc.sync.dma_start(
+                out=words[G].rearrange("p m t -> p (m t)").bitcast(I32), in_=o_codes[G][:].bitcast(I32)
+            )
+            for Q in range(4):
+                nc.sync.dma_start(
+                    out=scales[G, 4 * Q : 4 * Q + 4, :].bitcast(I32),
+                    in_=o_scales[G][32 * Q : 32 * Q + 4, :].bitcast(I32),
+                )
+
+        v_mult(0, 0)
+        v_mult(0, 1)
+        v_neg(0)
+        r_scaled(0)
+        v_mult(1, 0)
+        v_mult(1, 1)
+        turn(0, 0, 0)
+        turn(0, 0, 1)
+        v_quant(0, 0, 2)
+        v_neg(1)
+        x_quant(0, 0, 0)
+        turn(0, 0, 2)
+        turn(0, 0, 3)
+        v_quant(0, 2, 1)
+        x_quant(0, 0, 1)
+        turn(1, 0, 0)
+        turn(1, 0, 1)
+        v_quant(1, 0, 2)
+        x_quant(1, 0, 0)
+        turn(1, 0, 2)
+        turn(1, 0, 3)
+        v_quant(1, 2, 1)
+        x_quant(1, 0, 1)
+        t_weave(0, 0, 0, "V")
+        turn(0, 1, 0)
+        turn(0, 1, 1)
+        x_quant(0, 1, 0)
+        turn(0, 1, 2)
+        turn(0, 1, 3)
+        x_quant(0, 1, 1)
+        t_weave(1, 0, 0, "V")
+        turn(1, 1, 0)
+        turn(1, 1, 1)
+        x_quant(1, 1, 0)
+        turn(1, 1, 2)
+        turn(1, 1, 3)
+        stage1(0, 0, 0)
+        stage1(0, 0, 1)
+        x_quant(1, 1, 1)
+        squares(0, 0, 0)
+        squares(0, 0, 1)
+        r_scaled(1)
+        t_quant(0, 0, 0)
+        stage1(0, 1, 0)
+        stage1(0, 1, 1)
+        dev1(0, 0)
+        t_weave(0, 1, 0, "S")
+        t_quant(1, 0, 0)
+        dev2(0, 0)
+        squares(0, 1, 0)
+        squares(0, 1, 1)
+        stage1(1, 0, 0)
+        stage1(1, 0, 1)
+        t_weave(1, 1, 0, "S")
+        t_quant(0, 1, 0)
+        err(0, 0, 0)
+        err(0, 0, 1)
+        dev1(0, 1)
+        err_neg(0, 0)
+        dev2(0, 1)
+        err_quant(0, 0)
+        stage1(1, 1, 0)
+        stage1(1, 1, 1)
+        squares(1, 0, 0)
+        squares(1, 0, 1)
+        err(0, 1, 0)
+        err(0, 1, 1)
+        dev1(1, 0)
+        err_neg(0, 1)
+        t_quant(1, 1, 0)
+        squares(1, 1, 0)
+        squares(1, 1, 1)
+        dev2(1, 0)
+        err_quant(0, 1)
+        for t in range(4):
+            stage2(0, t, 0)
+        t_weave(0, 0, 1, "S")
+        err(1, 0, 0)
+        err(1, 0, 1)
+        dev1(1, 1)
+        err_neg(1, 0)
+        dev2(1, 1)
+        err_quant(1, 0)
+        t_weave(1, 0, 1, "S")
+        err(1, 1, 0)
+        err(1, 1, 1)
+        t_quant(0, 0, 1)
+        err_neg(1, 1)
+        t_weave(1, 1, 1, "V")
+        err_quant(1, 1)
+        for t in range(4):
+            stage2(0, t, 1)
+        t_quant(1, 0, 1)
+        for t in range(4):
+            stage2(1, t, 0)
+        t_weave(0, 1, 1, "S")
+        t_quant(1, 1, 1)
+        for t in range(4):
+            leave(0, t)
+        t_quant(0, 1, 1)
+        for t in range(4):
+            stage2(1, t, 1)
+        store_out(0)
+        out_weave(0, 0)
+        out_weave(0, 1)
+        out_quant(0, 0)
+        out_quant(0, 1)
+        store_planes(0)
+        for t in range(4):
+            leave(1, t)
+        store_out(1)
+        out_weave(1, 0)
+        out_weave(1, 1)
+        out_quant(1, 0)
+        out_quant(1, 1)
+        store_planes(1)

@@ -30,49 +30,54 @@ def tile_godardconstantmodulusgradient_x1_kernel(tc, y, w, q, a, r, out, words, 
 
         a_bf = kt("a_bf", [P, 2, 4], BF16)
         q_bf = kt("q_bf", [P, 2, 4], BF16)
-        r_bf = kt("r_bf", [P, J], BF16)
+        r_bf = kt("r_bf", [P, 2], BF16)
         nc.scalar.dma_start(out=a_bf[:], in_=a.rearrange("(g p j) -> p g j", p=P, j=4))
         nc.scalar.dma_start(out=q_bf[:], in_=q.rearrange("(g p j) -> p g j", p=P, j=4))
-        nc.scalar.dma_start(out=r_bf[:], in_=r.partition_broadcast(P))
-        w_raw = {}
-        for G in (0, 1):
-            w_raw[G] = kt("w_raw%d" % G, [P, 2, 4, J], BF16)
-            for c in (0, 1):
-                nc.sync.dma_start(
-                    out=w_raw[G][:, c],
-                    in_=w[c, 512 * G : 512 * G + 512, :].rearrange("(p j) n -> p j n", j=4),
-                )
-        y_raw = {}
-        for g in (0, 1):
-            for c in (0, 1):
-                y_raw[c, g] = kt("y_raw%d%d" % (c, g), [P, 4, D], BF16)
-                src = y[c, 512 * g : 512 * g + 512, :].rearrange("(p j) d -> p j d", j=4)
-                for j0 in (0, 2):
-                    nc.sync.dma_start(out=y_raw[c, g][:, j0 : j0 + 2], in_=src[:, j0 : j0 + 2])
+        nc.scalar.dma_start(out=r_bf[:], in_=r.rearrange("(p u) -> p u", u=2))
+        w_raw = {G: kt("w_raw%d" % G, [P, 2, 4, J], BF16) for G in (0, 1)}
+        y_raw = {(c, g): kt("y_raw%d%d" % (c, g), [P, 4, D], BF16) for c in (0, 1) for g in (0, 1)}
+
+        def load_w(G, c):
+            nc.sync.dma_start(
+                out=w_raw[G][:, c],
+                in_=w[c, 512 * G : 512 * G + 512, :].rearrange("(p j) n -> p j n", j=4),
+            )
+
+        def load_y(c, g):
+            src = y[c, 512 * g : 512 * g + 512, :].rearrange("(p j) d -> p j d", j=4)
+            for j0 in (0, 2):
+                nc.sync.dma_start(out=y_raw[c, g][:, j0 : j0 + 2], in_=src[:, j0 : j0 + 2])
+
+        load_w(0, 0)
+        load_w(0, 1)
+        load_y(0, 0)
+        load_w(1, 0)
+        load_w(1, 1)
+        load_y(1, 0)
+        load_y(0, 1)
+        load_y(1, 1)
 
         ident = kt("ident", [P, P], F32)
         make_identity(nc, ident[:])
 
         q2 = kt("q2", [P, 8], F32)
         s_col = kt("s_col", [P, 8], F32)
-        k_col = kt("k_col", [P, 8], F32)
+        nk_col = kt("nk_col", [P, 8], F32)
+        r_f = kt("r_f", [P, 2], F32)
+        r_b = kt("r_b", [P, J], F32)
         a_col = kt("a_col", [P, 8], F32)
         qv = q_bf[:].rearrange("p g j -> p (g j)")
         nc.vector.tensor_tensor(out=q2[:], in0=qv, in1=qv, op=ALU.mult)
         nc.vector.tensor_copy(out=a_col[:], in_=a_bf[:].rearrange("p g j -> p (g j)"))
-        nc.vector.tensor_scalar(out=k_col[:], in0=q2[:], scalar1=2.0**-5, scalar2=None, op0=ALU.mult)
+        nc.vector.tensor_copy(out=r_f[:], in_=r_bf[:])
+        nc.vector.tensor_scalar(out=nk_col[:], in0=q2[:], scalar1=-(2.0**-5), scalar2=None, op0=ALU.mult)
         nc.vector.tensor_scalar(out=s_col[:], in0=q2[:], scalar1=2.0**-2.5, scalar2=None, op0=ALU.mult)
 
-        rr = kt("rr", [P, 2, 2, 4, 128], F32)
-
-        def r_scaled(g):
-            for j in range(4):
-                nc.scalar.activation(
-                    out=rr[:, g, :, j, :],
-                    in_=r_bf[:].rearrange("p (h n) -> p h n", h=2),
-                    func=ACT.Copy,
-                    scale=k_col[:, 4 * g + j : 4 * g + j + 1],
-                )
+        def r_bcast():
+            rp = psum.tile([P, 2, P], F32, name="rp", tag="b0")
+            for u in (0, 1):
+                nc.tensor.transpose(rp[:, u, :], r_f[:, u : u + 1].to_broadcast([P, P]), ident[:])
+            nc.scalar.copy(out=r_b[:].rearrange("p (n u) -> p n u", u=2), in_=rp[:].rearrange("p u n -> p n u"))
 
         v_bf, v_codes, v_scales = {}, {}, {}
         for G in (0, 1):
@@ -88,15 +93,16 @@ def tile_godardconstantmodulusgradient_x1_kernel(tc, y, w, q, a, r, out, words, 
                 op=ALU.mult,
             )
 
-        def v_neg(G):
+        def v_neg(G, eng="V"):
             vi = v_bf[G][:, 1].rearrange("p n j -> p (n j)")
             vn = v_bf[G][:, 2].rearrange("p n j -> p (n j)")
-            if G == 0:
+            if eng == "S":
                 nc.scalar.activation(out=vn, in_=vi, func=ACT.Copy, scale=-1.0)
             else:
                 nc.vector.tensor_scalar(out=vn, in0=vi, scalar1=-1.0, scalar2=None, op0=ALU.mult)
 
-        def v_quant(G, lo, n):
+        def v_quant(G, lo):
+            n = 2 if lo == 0 else 1
             nc.vector.quantize_mx(
                 out=v_codes[G][:, lo * J : (lo + n) * J].bitcast(FP8X4),
                 scales=v_scales[G][:, lo * J : (lo + n) * J],
@@ -109,25 +115,28 @@ def tile_godardconstantmodulusgradient_x1_kernel(tc, y, w, q, a, r, out, words, 
                 x_codes[c, g] = kt("x_codes%d%d" % (c, g), [P, 4, 2, P], U32)
                 x_scales[c, g] = kt("x_scales%d%d" % (c, g), [P, 4, 2, P], U8)
 
-        bank_of_t = [0]
+        turns = []
 
-        def turn(c, g, j):
-            if j % 2 == 0:
-                yt[c, g] = stage.tile([P, 2, 2, P, 2], F32, name="yt", align_bytes=64)
-            b = bank_of_t[0] % 4
-            bank_of_t[0] += 1
-            tp = psum.tile([P, 2, 2, P], F32, name="tp", tag="b%d" % b)
+        def turn(c, g, j, eng="S"):
+            if (c, g, j // 2) not in yt:
+                yt[c, g, j // 2] = stage.tile([P, 2, 2, P, 2], F32, name="yt", align_bytes=64)
+            tp = psum.tile([P, 2, 2, P], F32, name="tp", tag="b%d" % (len(turns) % 4))
+            turns.append(j)
             wordsv = y_raw[c, g][:, j, :].bitcast(F32)
             for G in (0, 1):
                 for u in (0, 1):
                     nc.tensor.transpose(tp[:, G, u, :], wordsv[:, 256 * G + u : 256 * (G + 1) : 2], ident[:])
-            nc.scalar.copy(out=yt[c, g][:, j % 2], in_=tp[:].rearrange("p g u r -> p g r u"))
+            dst, src = yt[c, g, j // 2][:, j % 2], tp[:].rearrange("p g u r -> p g r u")
+            if eng == "S":
+                nc.scalar.copy(out=dst, in_=src)
+            else:
+                nc.vector.tensor_copy(out=dst, in_=src)
 
         def x_quant(c, g, h):
             nc.vector.quantize_mx(
                 out=x_codes[c, g][:, 2 * h : 2 * h + 2].rearrange("p j g r -> p (j g r)").bitcast(FP8X4),
                 scales=x_scales[c, g][:, 2 * h : 2 * h + 2].rearrange("p j g r -> p (j g r)"),
-                in_=yt[c, g][:].rearrange("p j g r u -> p (j g r u)").bitcast(BF16),
+                in_=yt[c, g, h][:].rearrange("p j g r u -> p (j g r u)").bitcast(BF16),
             )
 
         t_codes, t_scales, ti = {}, {}, {}
@@ -136,14 +145,16 @@ def tile_godardconstantmodulusgradient_x1_kernel(tc, y, w, q, a, r, out, words, 
                 t_codes[c, g] = kt("t_codes%d%d" % (c, g), [P, D], U32)
                 t_scales[c, g] = kt("t_scales%d%d" % (c, g), [P, D], U8)
 
-        def t_weave(c, g, G, eng):
-            t = stage.tile([P, 4, P, 4], BF16, name="ti", align_bytes=64)
-            ti[c, g, G] = t
-            src = y_raw[c, g][:, :, 512 * G : 512 * G + 512].rearrange("p j (m t) -> p t m j", t=4)
+        def t_weave(c, g, G, half, eng="V"):
+            if (c, g, G) not in ti:
+                ti[c, g, G] = stage.tile([P, 4, P, 4], BF16, name="ti", align_bytes=64, bufs=8)
+            m0 = 64 * half
+            dst = ti[c, g, G][:, :, m0 : m0 + 64, :].rearrange("p t m j -> p m j t")
+            src = y_raw[c, g][:, :, 512 * G + 4 * m0 : 512 * G + 4 * m0 + 256].rearrange("p j (m t) -> p m j t", t=4)
             if eng == "S":
-                nc.scalar.copy(out=t[:], in_=src)
+                nc.scalar.copy(out=dst, in_=src)
             else:
-                nc.vector.tensor_copy(out=t[:], in_=src)
+                nc.vector.tensor_copy(out=dst, in_=src)
 
         def t_quant(c, g, G):
             nc.vector.quantize_mx(
@@ -182,7 +193,7 @@ def tile_godardconstantmodulusgradient_x1_kernel(tc, y, w, q, a, r, out, words, 
                         n += 1
 
         def squares(g, h, x):
-            if x == 0:
+            if (g, h) not in sq:
                 sq[g, h] = stage.tile([P, 2, 4, P], F32, name="sq", align_bytes=64, bufs=2)
             for j in range(4):
                 nc.scalar.activation(
@@ -195,7 +206,15 @@ def tile_godardconstantmodulusgradient_x1_kernel(tc, y, w, q, a, r, out, words, 
         def dev1(g, h):
             u = stage.tile([P, 4, P], F32, name="u", align_bytes=64, bufs=2)
             dev[g, h, 0] = u
-            nc.vector.tensor_tensor(out=u[:], in0=sq[g, h][:, 0], in1=rr[:, g, h], op=ALU.subtract)
+            for j in range(4):
+                nc.vector.scalar_tensor_tensor(
+                    out=u[:, j, :],
+                    in0=r_b[:, 128 * h : 128 * h + 128],
+                    scalar=nk_col[:, 4 * g + j : 4 * g + j + 1],
+                    in1=sq[g, h][:, 0, j, :],
+                    op0=ALU.mult,
+                    op1=ALU.add,
+                )
 
         def dev2(g, h):
             m = stage.tile([P, 4, P], F32, name="m", align_bytes=64, bufs=2)
@@ -250,13 +269,32 @@ def tile_godardconstantmodulusgradient_x1_kernel(tc, y, w, q, a, r, out, words, 
                     stop=(g == 1 and c == 1),
                 )
 
-        def leave(G, t):
-            nc.scalar.activation(
-                out=res[G][:, :, t, :],
-                in_=acc[G, t][:].rearrange("p (c n) -> p c n", c=2),
-                func=ACT.Copy,
-                scale=a_col[:, 4 * G + t : 4 * G + t + 1],
-            )
+        def stage2h(G, t, c):
+            if c == 0:
+                acc[G, t] = psum.tile([P, 2 * J], F32, name="acc", tag="b%d" % ((4 if G == 0 else 0) + t))
+            lo = 512 * G + 128 * t
+            for g in (0, 1):
+                for part in (0, 1):
+                    nc.tensor.matmul_mx(
+                        out=acc[G, t][:, c * J : (c + 1) * J],
+                        lhsT=t_codes[part, g][:, lo : lo + 128].bitcast(FP8X4),
+                        lhsT_scale=t_scales[part, g][:, lo : lo + 128],
+                        rhs=e_codes[g][:, (c + part) * J : (c + part + 1) * J].bitcast(FP8X4),
+                        rhs_scale=e_scales[g][:, (c + part) * J : (c + part + 1) * J],
+                        start=(g == 0 and part == 0),
+                        stop=(g == 1 and part == 1),
+                    )
+
+        def leave(G, t, c, eng="S"):
+            if c == 2:
+                dst, src = res[G][:, :, t, :], acc[G, t][:].rearrange("p (c n) -> p c n", c=2)
+            else:
+                dst, src = res[G][:, c, t, :], acc[G, t][:, c * J : (c + 1) * J]
+            gain = a_col[:, 4 * G + t : 4 * G + t + 1]
+            if eng == "S":
+                nc.scalar.activation(out=dst, in_=src, func=ACT.Copy, scale=gain)
+            else:
+                nc.vector.tensor_scalar(out=dst, in0=src, scalar1=gain, scalar2=None, op0=ALU.mult)
 
         def out_weave(G, c):
             nc.vector.tensor_copy(
@@ -270,135 +308,166 @@ def tile_godardconstantmodulusgradient_x1_kernel(tc, y, w, q, a, r, out, words, 
                 in_=ob[G][:, c * J : (c + 1) * J, :].rearrange("p n t -> p (n t)"),
             )
 
-        def store_out(G):
-            for c in (0, 1):
-                nc.sync.dma_start(
-                    out=out[c, 512 * G : 512 * G + 512, :].rearrange("(p t) n -> p t n", t=4), in_=res[G][:, c]
-                )
-
-        def store_planes(G):
+        def store_out(G, c):
             nc.sync.dma_start(
-                out=words[G].rearrange("p m t -> p (m t)").bitcast(I32), in_=o_codes[G][:].bitcast(I32)
+                out=out[c, 512 * G : 512 * G + 512, :].rearrange("(p t) n -> p t n", t=4), in_=res[G][:, c]
             )
+
+        def store_words(G, lo, n):
+            nc.sync.dma_start(
+                out=words[G].rearrange("p m t -> p (m t)").bitcast(I32)[:, lo * J : (lo + n) * J],
+                in_=o_codes[G][:, lo * J : (lo + n) * J].bitcast(I32),
+            )
+
+        def store_scales(G):
             for Q in range(4):
-                nc.sync.dma_start(
+                eng = nc.sync if Q % 2 == 0 else nc.scalar
+                eng.dma_start(
                     out=scales[G, 4 * Q : 4 * Q + 4, :].bitcast(I32),
                     in_=o_scales[G][32 * Q : 32 * Q + 4, :].bitcast(I32),
                 )
 
+        r_bcast()
+        turn(0, 0, 0)
         v_mult(0, 0)
         v_mult(0, 1)
-        v_neg(0)
-        r_scaled(0)
-        v_mult(1, 0)
-        v_mult(1, 1)
-        turn(0, 0, 0)
+        v_quant(0, 0)
         turn(0, 0, 1)
-        v_quant(0, 0, 2)
-        v_neg(1)
-        x_quant(0, 0, 0)
+        t_weave(0, 0, 0, 0)
         turn(0, 0, 2)
+        t_weave(0, 0, 0, 1, "S")
+        v_mult(1, 0)
         turn(0, 0, 3)
-        v_quant(0, 2, 1)
-        x_quant(0, 0, 1)
-        turn(1, 0, 0)
         turn(1, 0, 1)
-        v_quant(1, 0, 2)
-        x_quant(1, 0, 0)
+        v_mult(1, 1)
+        turn(1, 0, 0)
+        v_neg(0)
+        v_quant(1, 0)
+        x_quant(0, 0, 0)
+        v_neg(1)
         turn(1, 0, 2)
+        x_quant(1, 0, 0)
+        v_quant(0, 2)
+        v_quant(1, 2)
         turn(1, 0, 3)
-        v_quant(1, 2, 1)
         x_quant(1, 0, 1)
-        t_weave(0, 0, 0, "V")
+        x_quant(0, 0, 1)
         turn(0, 1, 0)
         turn(0, 1, 1)
-        x_quant(0, 1, 0)
-        turn(0, 1, 2)
-        turn(0, 1, 3)
-        x_quant(0, 1, 1)
-        t_weave(1, 0, 0, "V")
-        turn(1, 1, 0)
-        turn(1, 1, 1)
-        x_quant(1, 1, 0)
-        turn(1, 1, 2)
-        turn(1, 1, 3)
-        stage1(0, 0, 0)
-        stage1(0, 0, 1)
-        x_quant(1, 1, 1)
-        squares(0, 0, 0)
-        squares(0, 0, 1)
-        r_scaled(1)
         t_quant(0, 0, 0)
+        t_weave(0, 1, 0, 0, "S")
+        turn(0, 1, 2)
+        t_weave(1, 1, 0, 0)
+        turn(0, 1, 3)
+        turn(1, 1, 0)
+        t_weave(0, 1, 0, 1)
+        t_weave(1, 1, 0, 1)
+        t_weave(0, 1, 1, 1)
+        turn(1, 1, 1)
         stage1(0, 1, 0)
-        stage1(0, 1, 1)
-        dev1(0, 0)
-        t_weave(0, 1, 0, "S")
-        t_quant(1, 0, 0)
-        dev2(0, 0)
-        squares(0, 1, 0)
-        squares(0, 1, 1)
-        stage1(1, 0, 0)
-        stage1(1, 0, 1)
-        t_weave(1, 1, 0, "S")
-        t_quant(0, 1, 0)
-        err(0, 0, 0)
-        err(0, 0, 1)
-        dev1(0, 1)
-        err_neg(0, 0)
-        dev2(0, 1)
-        err_quant(0, 0)
-        stage1(1, 1, 0)
-        stage1(1, 1, 1)
-        squares(1, 0, 0)
-        squares(1, 0, 1)
-        err(0, 1, 0)
-        err(0, 1, 1)
-        dev1(1, 0)
-        err_neg(0, 1)
+        x_quant(0, 1, 1)
+        x_quant(0, 1, 0)
+        stage1(0, 0, 0)
+        squares(0, 0, 0)
         t_quant(1, 1, 0)
+        turn(1, 1, 3)
+        turn(1, 1, 2)
+        squares(0, 1, 0)
+        stage1(0, 0, 1)
+        squares(0, 0, 1)
+        x_quant(1, 1, 0)
+        stage1(0, 1, 1)
+        x_quant(1, 1, 1)
+        squares(0, 1, 1)
+        t_weave(1, 0, 0, 0, "S")
+        stage1(1, 0, 0)
+        t_weave(1, 0, 0, 1, "S")
+        dev1(0, 1)
+        t_weave(1, 0, 1, 0)
+        dev1(0, 0)
+        dev2(0, 1)
+        dev2(0, 0)
+        stage1(1, 1, 0)
+        t_quant(0, 1, 0)
+        stage1(1, 0, 1)
+        squares(1, 0, 0)
+        err(0, 1, 0)
+        err(0, 0, 0)
         squares(1, 1, 0)
+        err(0, 0, 1)
+        t_quant(1, 0, 0)
+        dev1(1, 1)
+        dev1(1, 0)
+        stage1(1, 1, 1)
+        squares(1, 0, 1)
+        err_neg(0, 0)
+        err_neg(0, 1)
+        t_weave(1, 1, 1, 0, "S")
         squares(1, 1, 1)
         dev2(1, 0)
-        err_quant(0, 1)
-        for t in range(4):
-            stage2(0, t, 0)
-        t_weave(0, 0, 1, "S")
-        err(1, 0, 0)
-        err(1, 0, 1)
-        dev1(1, 1)
-        err_neg(1, 0)
+        err(0, 1, 1)
         dev2(1, 1)
-        err_quant(1, 0)
-        t_weave(1, 0, 1, "S")
+        err_quant(0, 1)
+        err(1, 0, 0)
+        t_weave(0, 0, 1, 1, "S")
+        t_weave(1, 0, 1, 1, "S")
         err(1, 1, 0)
+        err_quant(0, 0)
+        stage2(0, 1, 0)
+        t_weave(1, 1, 1, 1, "S")
+        t_weave(0, 1, 1, 0, "S")
+        err_neg(1, 0)
         err(1, 1, 1)
-        t_quant(0, 0, 1)
+        stage2(0, 0, 0)
+        stage2(0, 2, 0)
+        stage2(0, 3, 0)
+        t_weave(0, 0, 1, 0, "S")
         err_neg(1, 1)
-        t_weave(1, 1, 1, "V")
+        err(1, 0, 1)
         err_quant(1, 1)
-        for t in range(4):
-            stage2(0, t, 1)
+        err_quant(1, 0)
+        stage2(0, 3, 1)
+        stage2(0, 1, 1)
+        leave(0, 1, 2)
         t_quant(1, 0, 1)
-        for t in range(4):
-            stage2(1, t, 0)
-        t_weave(0, 1, 1, "S")
         t_quant(1, 1, 1)
-        for t in range(4):
-            leave(0, t)
         t_quant(0, 1, 1)
-        for t in range(4):
-            stage2(1, t, 1)
-        store_out(0)
+        stage2(0, 2, 1)
+        stage2(0, 0, 1)
+        t_quant(0, 0, 1)
+        leave(0, 0, 2, "V")
+        stage2h(1, 2, 0)
+        leave(0, 3, 2)
+        stage2h(1, 0, 0)
+        stage2h(1, 3, 0)
+        leave(0, 2, 2)
+        store_out(0, 0)
+        store_out(0, 1)
         out_weave(0, 0)
+        leave(1, 0, 0)
+        stage2h(1, 1, 0)
+        stage2h(1, 2, 1)
+        leave(1, 2, 1)
+        leave(1, 2, 0, "V")
+        leave(1, 3, 0)
         out_weave(0, 1)
-        out_quant(0, 0)
+        leave(1, 1, 0, "V")
+        store_out(1, 0)
         out_quant(0, 1)
-        store_planes(0)
-        for t in range(4):
-            leave(1, t)
-        store_out(1)
+        stage2h(1, 1, 1)
+        leave(1, 1, 1)
+        stage2h(1, 3, 1)
+        stage2h(1, 0, 1)
+        out_quant(0, 0)
+        store_words(0, 0, 2)
+        store_scales(0)
+        leave(1, 3, 1)
         out_weave(1, 0)
-        out_weave(1, 1)
+        leave(1, 0, 1)
+        store_out(1, 1)
         out_quant(1, 0)
+        store_words(1, 0, 1)
+        out_weave(1, 1)
         out_quant(1, 1)
-        store_planes(1)
+        store_words(1, 1, 1)
+        store_scales(1)

@@ -60,6 +60,24 @@ def tile_godardconstantmodulusgradient_x1_kernel(tc, y, w, q, a, r, out, words, 
         ident = kt("ident", [P, P], F32)
         make_identity(nc, ident[:])
 
+        w1_bf = kt("w1_bf", [P, 2048], BF16)
+        w1_codes = kt("w1_codes", [P, 512], U32)
+        w1_scales = kt("w1_scales", [P, 512], U8)
+        nc.vector.memset(w1_bf[:], 0.0)
+        nc.vector.quantize_mx(out=w1_codes[:].bitcast(FP8X4), scales=w1_scales[:], in_=w1_bf[:])
+
+        def warm(i):
+            wt = psum.tile([P, 512], F32, name="wt", tag="b7")
+            nc.tensor.matmul_mx(
+                out=wt[:],
+                lhsT=w1_codes[:, 0:128].bitcast(FP8X4),
+                lhsT_scale=w1_scales[:, 0:128],
+                rhs=w1_codes[:].bitcast(FP8X4),
+                rhs_scale=w1_scales[:],
+                start=True,
+                stop=True,
+            )
+
         q2 = kt("q2", [P, 8], F32)
         s_col = kt("s_col", [P, 8], F32)
         nk_col = kt("nk_col", [P, 8], F32)
@@ -85,11 +103,11 @@ def tile_godardconstantmodulusgradient_x1_kernel(tc, y, w, q, a, r, out, words, 
             v_codes[G] = kt("v_codes%d" % G, [P, 3 * J], U32)
             v_scales[G] = kt("v_scales%d" % G, [P, 3 * J], U8)
 
-        def v_mult(G, c):
+        def v_mult(G):
             nc.vector.tensor_tensor(
-                out=v_bf[G][:, c],
-                in0=w_raw[G][:, c].rearrange("p j n -> p n j"),
-                in1=a_bf[:, G, :].unsqueeze(1).to_broadcast([P, J, 4]),
+                out=v_bf[G][:, 0:2],
+                in0=w_raw[G][:].rearrange("p c j n -> p c n j"),
+                in1=a_bf[:, G, :].unsqueeze(1).unsqueeze(1).to_broadcast([P, 2, J, 4]),
                 op=ALU.mult,
             )
 
@@ -145,16 +163,21 @@ def tile_godardconstantmodulusgradient_x1_kernel(tc, y, w, q, a, r, out, words, 
                 t_codes[c, g] = kt("t_codes%d%d" % (c, g), [P, D], U32)
                 t_scales[c, g] = kt("t_scales%d%d" % (c, g), [P, D], U8)
 
-        def t_weave(c, g, G, half, eng="V"):
-            if (c, g, G) not in ti:
-                ti[c, g, G] = stage.tile([P, 4, P, 4], BF16, name="ti", align_bytes=64, bufs=8)
-            m0 = 64 * half
-            dst = ti[c, g, G][:, :, m0 : m0 + 64, :].rearrange("p t m j -> p m j t")
-            src = y_raw[c, g][:, :, 512 * G + 4 * m0 : 512 * G + 4 * m0 + 256].rearrange("p j (m t) -> p m j t", t=4)
+        def weave_part(c, g, G, m0, n, eng):
+            dst = ti[c, g, G][:, :, m0 : m0 + n, :].rearrange("p t m j -> p m j t")
+            src = y_raw[c, g][:, :, 512 * G + 4 * m0 : 512 * G + 4 * (m0 + n)].rearrange("p j (m t) -> p m j t", t=4)
             if eng == "S":
                 nc.scalar.copy(out=dst, in_=src)
             else:
                 nc.vector.tensor_copy(out=dst, in_=src)
+
+        def t_weave(c, g, G, eng):
+            ti[c, g, G] = stage.tile([P, 4, P, 4], BF16, name="ti", align_bytes=64, bufs=8)
+            if eng == "V":
+                weave_part(c, g, G, 0, 128, "V")
+            else:
+                weave_part(c, g, G, 0, 64, "S" if eng == "S" else "V")
+                weave_part(c, g, G, 64, 64, "S")
 
         def t_quant(c, g, G):
             nc.vector.quantize_mx(
@@ -230,22 +253,29 @@ def tile_godardconstantmodulusgradient_x1_kernel(tc, y, w, q, a, r, out, words, 
             )
 
         def err_neg(g, h):
+            lo, n = (0, J) if h == 2 else (128 * h, 128)
             nc.vector.tensor_scalar(
-                out=e_bf[g][:, 2, 128 * h : 128 * h + 128, :].rearrange("p n j -> p (n j)"),
-                in0=e_bf[g][:, 0, 128 * h : 128 * h + 128, :].rearrange("p n j -> p (n j)"),
+                out=e_bf[g][:, 2, lo : lo + n, :].rearrange("p n j -> p (n j)"),
+                in0=e_bf[g][:, 0, lo : lo + n, :].rearrange("p n j -> p (n j)"),
                 scalar1=-1.0,
                 scalar2=None,
                 op0=ALU.mult,
             )
 
+        def quant_err(g, lo, n):
+            nc.vector.quantize_mx(
+                out=e_codes[g][:, lo : lo + n].bitcast(FP8X4),
+                scales=e_scales[g][:, lo : lo + n],
+                in_=e_bf[g][:].rearrange("p x n j -> p (x n j)")[:, 4 * lo : 4 * (lo + n)],
+            )
+
         def err_quant(g, h):
-            for x in (0, 1, 2):
-                lo = x * J + 128 * h
-                nc.vector.quantize_mx(
-                    out=e_codes[g][:, lo : lo + 128].bitcast(FP8X4),
-                    scales=e_scales[g][:, lo : lo + 128],
-                    in_=e_bf[g][:, x, 128 * h : 128 * h + 128, :].rearrange("p n j -> p (n j)"),
-                )
+            if h == 2:
+                quant_err(g, 0, 2 * J)
+                quant_err(g, 2 * J, J)
+            else:
+                for x in (0, 1, 2):
+                    quant_err(g, x * J + 128 * h, 128)
 
         acc, res, ob, o_codes, o_scales = {}, {}, {}, {}, {}
         for G in (0, 1):
@@ -297,15 +327,18 @@ def tile_godardconstantmodulusgradient_x1_kernel(tc, y, w, q, a, r, out, words, 
                 nc.vector.tensor_scalar(out=dst, in0=src, scalar1=gain, scalar2=None, op0=ALU.mult)
 
         def out_weave(G, c):
+            cs = slice(0, 2) if c == 2 else slice(c, c + 1)
             nc.vector.tensor_copy(
-                out=ob[G][:, c * J : (c + 1) * J, :], in_=res[G][:, c].rearrange("p t n -> p n t")
+                out=ob[G][:].rearrange("p (c n) t -> p c n t", c=2)[:, cs],
+                in_=res[G][:, cs].rearrange("p c t n -> p c n t"),
             )
 
         def out_quant(G, c):
+            lo, n = (0, 2 * J) if c == 2 else (c * J, J)
             nc.vector.quantize_mx(
-                out=o_codes[G][:, c * J : (c + 1) * J].bitcast(FP8X4),
-                scales=o_scales[G][:, c * J : (c + 1) * J],
-                in_=ob[G][:, c * J : (c + 1) * J, :].rearrange("p n t -> p (n t)"),
+                out=o_codes[G][:, lo : lo + n].bitcast(FP8X4),
+                scales=o_scales[G][:, lo : lo + n],
+                in_=ob[G][:, lo : lo + n, :].rearrange("p n t -> p (n t)"),
             )
 
         def store_out(G, c):
@@ -327,146 +360,140 @@ def tile_godardconstantmodulusgradient_x1_kernel(tc, y, w, q, a, r, out, words, 
                     in_=o_scales[G][32 * Q : 32 * Q + 4, :].bitcast(I32),
                 )
 
+        warm(0)
+        warm(1)
+        warm(2)
+        warm(3)
+        warm(4)
+        warm(5)
+        warm(6)
+        warm(7)
         r_bcast()
-        turn(0, 0, 0)
-        v_mult(0, 0)
-        v_mult(0, 1)
-        v_quant(0, 0)
-        turn(0, 0, 1)
-        t_weave(0, 0, 0, 0)
-        turn(0, 0, 2)
-        t_weave(0, 0, 0, 1, "S")
-        v_mult(1, 0)
-        turn(0, 0, 3)
-        turn(1, 0, 1)
-        v_mult(1, 1)
-        turn(1, 0, 0)
+        v_mult(0)
         v_neg(0)
-        v_quant(1, 0)
+        v_quant(0, 0)
+        turn(0, 0, 0)
+        turn(0, 0, 1)
+        v_mult(1)
         x_quant(0, 0, 0)
-        v_neg(1)
-        turn(1, 0, 2)
-        x_quant(1, 0, 0)
-        v_quant(0, 2)
-        v_quant(1, 2)
-        turn(1, 0, 3)
-        x_quant(1, 0, 1)
-        x_quant(0, 0, 1)
-        turn(0, 1, 0)
-        turn(0, 1, 1)
+        t_weave(0, 0, 0, "S")
+        turn(0, 0, 2)
         t_quant(0, 0, 0)
-        t_weave(0, 1, 0, 0, "S")
+        v_quant(1, 0)
+        v_neg(1)
+        turn(0, 0, 3)
+        x_quant(0, 0, 1)
+        turn(1, 0, 1)
+        turn(1, 0, 3)
+        turn(1, 0, 0)
+        v_quant(1, 2)
+        turn(1, 0, 2)
+        t_weave(1, 0, 1, "S")
+        x_quant(1, 0, 0)
         turn(0, 1, 2)
-        t_weave(1, 1, 0, 0)
-        turn(0, 1, 3)
-        turn(1, 1, 0)
-        t_weave(0, 1, 0, 1)
-        t_weave(1, 1, 0, 1)
-        t_weave(0, 1, 1, 1)
         turn(1, 1, 1)
-        stage1(0, 1, 0)
-        x_quant(0, 1, 1)
-        x_quant(0, 1, 0)
+        v_quant(0, 2)
+        x_quant(1, 0, 1)
         stage1(0, 0, 0)
         squares(0, 0, 0)
-        t_quant(1, 1, 0)
-        turn(1, 1, 3)
+        t_weave(0, 0, 1, "V")
+        turn(0, 1, 3)
+        turn(1, 1, 0)
+        t_weave(1, 0, 0, "V")
+        t_weave(1, 1, 0, "H")
         turn(1, 1, 2)
-        squares(0, 1, 0)
         stage1(0, 0, 1)
-        squares(0, 0, 1)
-        x_quant(1, 1, 0)
-        stage1(0, 1, 1)
-        x_quant(1, 1, 1)
-        squares(0, 1, 1)
-        t_weave(1, 0, 0, 0, "S")
-        stage1(1, 0, 0)
-        t_weave(1, 0, 0, 1, "S")
-        dev1(0, 1)
-        t_weave(1, 0, 1, 0)
-        dev1(0, 0)
-        dev2(0, 1)
-        dev2(0, 0)
-        stage1(1, 1, 0)
-        t_quant(0, 1, 0)
-        stage1(1, 0, 1)
-        squares(1, 0, 0)
-        err(0, 1, 0)
-        err(0, 0, 0)
-        squares(1, 1, 0)
-        err(0, 0, 1)
         t_quant(1, 0, 0)
-        dev1(1, 1)
-        dev1(1, 0)
-        stage1(1, 1, 1)
+        dev1(0, 0)
+        x_quant(0, 1, 1)
+        turn(0, 1, 1)
+        t_quant(0, 0, 1)
+        x_quant(1, 1, 0)
+        turn(1, 1, 3, "V")
+        t_quant(1, 1, 0)
+        turn(0, 1, 0)
+        x_quant(1, 1, 1)
+        squares(0, 0, 1)
+        x_quant(0, 1, 0)
+        dev2(0, 0)
+        stage1(0, 1, 0)
+        stage1(0, 1, 1)
+        squares(0, 1, 0)
+        stage1(1, 0, 0)
+        dev1(0, 1)
+        stage1(1, 0, 1)
+        squares(0, 1, 1)
+        stage1(1, 1, 0)
+        squares(1, 0, 0)
         squares(1, 0, 1)
-        err_neg(0, 0)
-        err_neg(0, 1)
-        t_weave(1, 1, 1, 0, "S")
-        squares(1, 1, 1)
+        err(0, 0, 1)
+        dev2(0, 1)
+        squares(1, 1, 0)
+        err(0, 0, 0)
+        stage1(1, 1, 1)
+        err(0, 1, 0)
+        dev1(1, 0)
+        err_neg(0, 2)
         dev2(1, 0)
+        squares(1, 1, 1)
         err(0, 1, 1)
-        dev2(1, 1)
-        err_quant(0, 1)
         err(1, 0, 0)
-        t_weave(0, 0, 1, 1, "S")
-        t_weave(1, 0, 1, 1, "S")
-        err(1, 1, 0)
-        err_quant(0, 0)
-        stage2(0, 1, 0)
-        t_weave(1, 1, 1, 1, "S")
-        t_weave(0, 1, 1, 0, "S")
+        dev1(1, 1)
+        err_quant(0, 2)
+        dev2(1, 1)
+        t_weave(0, 1, 0, "S")
         err_neg(1, 0)
-        err(1, 1, 1)
-        stage2(0, 0, 0)
-        stage2(0, 2, 0)
-        stage2(0, 3, 0)
-        t_weave(0, 0, 1, 0, "S")
-        err_neg(1, 1)
         err(1, 0, 1)
-        err_quant(1, 1)
+        err(1, 1, 0)
+        stage2(0, 0, 0)
+        t_weave(0, 1, 1, "S")
         err_quant(1, 0)
-        stage2(0, 3, 1)
+        stage2(0, 3, 0)
+        err(1, 1, 1)
+        err_neg(1, 1)
+        t_quant(0, 1, 0)
+        stage2(0, 2, 0)
+        err_quant(1, 1)
+        t_weave(1, 1, 1, "H")
+        stage2(0, 1, 0)
+        t_quant(0, 1, 1)
         stage2(0, 1, 1)
+        stage2(0, 3, 1)
+        stage2(0, 0, 1)
+        stage2(0, 2, 1)
         leave(0, 1, 2)
         t_quant(1, 0, 1)
         t_quant(1, 1, 1)
-        t_quant(0, 1, 1)
-        stage2(0, 2, 1)
-        stage2(0, 0, 1)
-        t_quant(0, 0, 1)
-        leave(0, 0, 2, "V")
-        stage2h(1, 2, 0)
-        leave(0, 3, 2)
         stage2h(1, 0, 0)
+        stage2h(1, 1, 0)
+        stage2h(1, 1, 1)
         stage2h(1, 3, 0)
-        leave(0, 2, 2)
+        leave(0, 0, 2)
+        leave(0, 3, 2)
+        leave(0, 2, 2, "V")
         store_out(0, 0)
         store_out(0, 1)
-        out_weave(0, 0)
-        leave(1, 0, 0)
-        stage2h(1, 1, 0)
-        stage2h(1, 2, 1)
-        leave(1, 2, 1)
-        leave(1, 2, 0, "V")
-        leave(1, 3, 0)
-        out_weave(0, 1)
-        leave(1, 1, 0, "V")
-        store_out(1, 0)
-        out_quant(0, 1)
-        stage2h(1, 1, 1)
-        leave(1, 1, 1)
+        stage2h(1, 2, 0)
         stage2h(1, 3, 1)
-        stage2h(1, 0, 1)
-        out_quant(0, 0)
+        out_weave(0, 2)
+        out_quant(0, 2)
         store_words(0, 0, 2)
         store_scales(0)
-        leave(1, 3, 1)
+        stage2h(1, 0, 1)
+        leave(1, 3, 0, "V")
+        leave(1, 1, 0)
+        leave(1, 0, 0)
+        leave(1, 2, 0)
+        store_out(1, 0)
+        leave(1, 1, 1)
         out_weave(1, 0)
-        leave(1, 0, 1)
-        store_out(1, 1)
+        leave(1, 3, 1)
         out_quant(1, 0)
         store_words(1, 0, 1)
+        stage2h(1, 2, 1)
+        leave(1, 0, 1)
+        leave(1, 2, 1)
+        store_out(1, 1)
         out_weave(1, 1)
         out_quant(1, 1)
         store_words(1, 1, 1)

@@ -34,7 +34,7 @@ def tile_godardconstantmodulusgradient_x1_kernel(tc, y, w, q, a, r, out, words, 
         nc.scalar.dma_start(out=a_bf[:], in_=a.rearrange("(g p j) -> p g j", p=P, j=4))
         nc.scalar.dma_start(out=q_bf[:], in_=q.rearrange("(g p j) -> p g j", p=P, j=4))
         nc.scalar.dma_start(out=r_bf[:], in_=r.rearrange("(p u) -> p u", u=2))
-        w_raw = {G: kt("w_raw%d" % G, [P, 2, 4, J], BF16) for G in (0, 1)}
+        w_raw = {G: keep.tile([P, 2, 4, J], BF16, name="w_raw%d" % G, tag="wo%d" % G, align_bytes=64) for G in (0, 1)}
         y_raw = {(c, g): kt("y_raw%d%d" % (c, g), [P, 4, D], BF16) for c in (0, 1) for g in (0, 1)}
 
         def load_w(G, c):
@@ -60,14 +60,15 @@ def tile_godardconstantmodulusgradient_x1_kernel(tc, y, w, q, a, r, out, words, 
         ident = kt("ident", [P, P], F32)
         make_identity(nc, ident[:])
 
-        w1_bf = kt("w1_bf", [P, 2048], BF16)
-        w1_codes = kt("w1_codes", [P, 512], U32)
-        w1_scales = kt("w1_scales", [P, 512], U8)
-        nc.vector.memset(w1_bf[:], 0.0)
-        nc.vector.quantize_mx(out=w1_codes[:].bitcast(FP8X4), scales=w1_scales[:], in_=w1_bf[:])
+        w1_bf = stage.tile([P, 2, 4, P, 4], BF16, name="ti", align_bytes=64, bufs=4)
+        w1_codes = kt("w1_codes", [P, 256], U32)
+        w1_scales = kt("w1_scales", [P, 256], U8)
+        w1_in = w1_bf[:, 0, 0:2].rearrange("p t m j -> p (t m j)")
+        nc.vector.memset(w1_in, 0.0)
+        nc.vector.quantize_mx(out=w1_codes[:].bitcast(FP8X4), scales=w1_scales[:], in_=w1_in)
 
         def warm(i):
-            wt = psum.tile([P, 512], F32, name="wt", tag="b7")
+            wt = psum.tile([P, 256], F32, name="wt", tag="b7")
             nc.tensor.matmul_mx(
                 out=wt[:],
                 lhsT=w1_codes[:, 0:128].bitcast(FP8X4),
@@ -78,24 +79,32 @@ def tile_godardconstantmodulusgradient_x1_kernel(tc, y, w, q, a, r, out, words, 
                 stop=True,
             )
 
-        q2 = kt("q2", [P, 8], F32)
-        s_col = kt("s_col", [P, 8], F32)
-        nk_col = kt("nk_col", [P, 8], F32)
         r_f = kt("r_f", [P, 2], F32)
         r_b = kt("r_b", [P, J], F32)
+        k_col = kt("k_col", [P, 8], F32)
+        s_col = kt("s_col", [P, 8], F32)
         a_col = kt("a_col", [P, 8], F32)
-        qv = q_bf[:].rearrange("p g j -> p (g j)")
-        nc.vector.tensor_tensor(out=q2[:], in0=qv, in1=qv, op=ALU.mult)
-        nc.vector.tensor_copy(out=a_col[:], in_=a_bf[:].rearrange("p g j -> p (g j)"))
-        nc.vector.tensor_copy(out=r_f[:], in_=r_bf[:])
-        nc.vector.tensor_scalar(out=nk_col[:], in0=q2[:], scalar1=-(2.0**-5), scalar2=None, op0=ALU.mult)
-        nc.vector.tensor_scalar(out=s_col[:], in0=q2[:], scalar1=2.0**-2.5, scalar2=None, op0=ALU.mult)
+        rr = kt("rr", [P, 2, 2, 4, P], F32)
+        q_flat = q_bf[:].rearrange("p g j -> p (g j)")
+        nc.scalar.copy(out=r_f[:], in_=r_bf[:])
+        nc.scalar.activation(out=k_col[:], in_=q_flat, func=ACT.Square, scale=2.0**-2.5)
+        nc.scalar.activation(out=s_col[:], in_=q_flat, func=ACT.Square, scale=2.0**-1.25)
+        nc.scalar.copy(out=a_col[:], in_=a_bf[:].rearrange("p g j -> p (g j)"))
 
         def r_bcast():
             rp = psum.tile([P, 2, P], F32, name="rp", tag="b0")
             for u in (0, 1):
                 nc.tensor.transpose(rp[:, u, :], r_f[:, u : u + 1].to_broadcast([P, P]), ident[:])
             nc.scalar.copy(out=r_b[:].rearrange("p (n u) -> p n u", u=2), in_=rp[:].rearrange("p u n -> p n u"))
+
+        def r_scaled(g):
+            for j in range(4):
+                nc.scalar.activation(
+                    out=rr[:, g, :, j, :],
+                    in_=r_b[:].rearrange("p (h n) -> p h n", h=2),
+                    func=ACT.Copy,
+                    scale=k_col[:, 4 * g + j : 4 * g + j + 1],
+                )
 
         v_bf, v_codes, v_scales = {}, {}, {}
         for G in (0, 1):
@@ -104,12 +113,14 @@ def tile_godardconstantmodulusgradient_x1_kernel(tc, y, w, q, a, r, out, words, 
             v_scales[G] = kt("v_scales%d" % G, [P, 3 * J], U8)
 
         def v_mult(G):
-            nc.vector.tensor_tensor(
-                out=v_bf[G][:, 0:2],
-                in0=w_raw[G][:].rearrange("p c j n -> p c n j"),
-                in1=a_bf[:, G, :].unsqueeze(1).unsqueeze(1).to_broadcast([P, 2, J, 4]),
-                op=ALU.mult,
-            )
+            for cs in ((slice(0, 1), slice(1, 2)) if G == 0 else (slice(0, 2),)):
+                n = cs.stop - cs.start
+                nc.vector.tensor_tensor(
+                    out=v_bf[G][:, cs],
+                    in0=w_raw[G][:, cs].rearrange("p c j n -> p c n j"),
+                    in1=a_bf[:, G, :].unsqueeze(1).unsqueeze(1).to_broadcast([P, n, J, 4]),
+                    op=ALU.mult,
+                )
 
         def v_neg(G, eng="V"):
             vi = v_bf[G][:, 1].rearrange("p n j -> p (n j)")
@@ -164,7 +175,7 @@ def tile_godardconstantmodulusgradient_x1_kernel(tc, y, w, q, a, r, out, words, 
                 t_scales[c, g] = kt("t_scales%d%d" % (c, g), [P, D], U8)
 
         def weave_part(c, g, G, m0, n, eng):
-            dst = ti[c, g, G][:, :, m0 : m0 + n, :].rearrange("p t m j -> p m j t")
+            dst = ti[c, g][:, G, :, m0 : m0 + n, :].rearrange("p t m j -> p m j t")
             src = y_raw[c, g][:, :, 512 * G + 4 * m0 : 512 * G + 4 * (m0 + n)].rearrange("p j (m t) -> p m j t", t=4)
             if eng == "S":
                 nc.scalar.copy(out=dst, in_=src)
@@ -172,7 +183,8 @@ def tile_godardconstantmodulusgradient_x1_kernel(tc, y, w, q, a, r, out, words, 
                 nc.vector.tensor_copy(out=dst, in_=src)
 
         def t_weave(c, g, G, eng):
-            ti[c, g, G] = stage.tile([P, 4, P, 4], BF16, name="ti", align_bytes=64, bufs=8)
+            if (c, g) not in ti:
+                ti[c, g] = stage.tile([P, 2, 4, P, 4], BF16, name="ti", align_bytes=64, bufs=4)
             if eng == "V":
                 weave_part(c, g, G, 0, 128, "V")
             else:
@@ -180,10 +192,11 @@ def tile_godardconstantmodulusgradient_x1_kernel(tc, y, w, q, a, r, out, words, 
                 weave_part(c, g, G, 64, 64, "S")
 
         def t_quant(c, g, G):
+            lo, n = (0, D) if G == 2 else (512 * G, 512)
             nc.vector.quantize_mx(
-                out=t_codes[c, g][:, 512 * G : 512 * G + 512].bitcast(FP8X4),
-                scales=t_scales[c, g][:, 512 * G : 512 * G + 512],
-                in_=ti[c, g, G][:].rearrange("p t m j -> p (t m j)"),
+                out=t_codes[c, g][:, lo : lo + n].bitcast(FP8X4),
+                scales=t_scales[c, g][:, lo : lo + n],
+                in_=ti[c, g][:].rearrange("p g t m j -> p (g t m j)")[:, 4 * lo : 4 * (lo + n)],
             )
 
         z = {}
@@ -229,26 +242,23 @@ def tile_godardconstantmodulusgradient_x1_kernel(tc, y, w, q, a, r, out, words, 
         def dev1(g, h):
             u = stage.tile([P, 4, P], F32, name="u", align_bytes=64, bufs=2)
             dev[g, h, 0] = u
-            for j in range(4):
-                nc.vector.scalar_tensor_tensor(
-                    out=u[:, j, :],
-                    in0=r_b[:, 128 * h : 128 * h + 128],
-                    scalar=nk_col[:, 4 * g + j : 4 * g + j + 1],
-                    in1=sq[g, h][:, 0, j, :],
-                    op0=ALU.mult,
-                    op1=ALU.add,
-                )
+            nc.vector.tensor_tensor(out=u[:], in0=sq[g, h][:, 0], in1=rr[:, g, h], op=ALU.subtract)
 
         def dev2(g, h):
-            m = stage.tile([P, 4, P], F32, name="m", align_bytes=64, bufs=2)
+            m = stage.tile([P, P, 4], F32, name="m", align_bytes=64, bufs=2)
             dev[g, h, 1] = m
-            nc.vector.tensor_tensor(out=m[:], in0=dev[g, h, 0][:], in1=sq[g, h][:, 1], op=ALU.add)
+            nc.vector.tensor_tensor(
+                out=m[:],
+                in0=dev[g, h, 0][:].rearrange("p j n -> p n j"),
+                in1=sq[g, h][:, 1].rearrange("p j n -> p n j"),
+                op=ALU.add,
+            )
 
         def err(g, h, x):
             nc.vector.tensor_tensor(
                 out=e_bf[g][:, x, 128 * h : 128 * h + 128, :],
                 in0=z[g, h, x][:].rearrange("p j n -> p n j"),
-                in1=dev[g, h, 1][:].rearrange("p j n -> p n j"),
+                in1=dev[g, h, 1][:],
                 op=ALU.mult,
             )
 
@@ -280,7 +290,6 @@ def tile_godardconstantmodulusgradient_x1_kernel(tc, y, w, q, a, r, out, words, 
         acc, res, ob, o_codes, o_scales = {}, {}, {}, {}, {}
         for G in (0, 1):
             res[G] = kt("res%d" % G, [P, 2, 4, J], F32)
-            ob[G] = kt("ob%d" % G, [P, 2 * J, 4], BF16)
             o_codes[G] = kt("o_codes%d" % G, [P, 2 * J], U32)
             o_scales[G] = kt("o_scales%d" % G, [P, 2 * J], U8)
 
@@ -327,6 +336,8 @@ def tile_godardconstantmodulusgradient_x1_kernel(tc, y, w, q, a, r, out, words, 
                 nc.vector.tensor_scalar(out=dst, in0=src, scalar1=gain, scalar2=None, op0=ALU.mult)
 
         def out_weave(G, c):
+            if G not in ob:
+                ob[G] = keep.tile([P, 2 * J, 4], BF16, name="ob%d" % G, tag="wo%d" % G, align_bytes=64)
             cs = slice(0, 2) if c == 2 else slice(c, c + 1)
             nc.vector.tensor_copy(
                 out=ob[G][:].rearrange("p (c n) t -> p c n t", c=2)[:, cs],
@@ -365,133 +376,140 @@ def tile_godardconstantmodulusgradient_x1_kernel(tc, y, w, q, a, r, out, words, 
         warm(2)
         warm(3)
         warm(4)
+        r_bcast()
         warm(5)
         warm(6)
         warm(7)
-        r_bcast()
-        v_mult(0)
-        v_neg(0)
-        v_quant(0, 0)
+        warm(8)
+        r_scaled(0)
         turn(0, 0, 0)
         turn(0, 0, 1)
-        v_mult(1)
-        x_quant(0, 0, 0)
-        t_weave(0, 0, 0, "S")
         turn(0, 0, 2)
-        t_quant(0, 0, 0)
-        v_quant(1, 0)
-        v_neg(1)
-        turn(0, 0, 3)
-        x_quant(0, 0, 1)
-        turn(1, 0, 1)
-        turn(1, 0, 3)
-        turn(1, 0, 0)
-        v_quant(1, 2)
-        turn(1, 0, 2)
-        t_weave(1, 0, 1, "S")
-        x_quant(1, 0, 0)
-        turn(0, 1, 2)
-        turn(1, 1, 1)
-        v_quant(0, 2)
-        x_quant(1, 0, 1)
-        stage1(0, 0, 0)
-        squares(0, 0, 0)
+        v_mult(0)
+        v_quant(0, 0)
         t_weave(0, 0, 1, "V")
-        turn(0, 1, 3)
-        turn(1, 1, 0)
-        t_weave(1, 0, 0, "V")
-        t_weave(1, 1, 0, "H")
-        turn(1, 1, 2)
-        stage1(0, 0, 1)
-        t_quant(1, 0, 0)
-        dev1(0, 0)
-        x_quant(0, 1, 1)
-        turn(0, 1, 1)
+        turn(0, 0, 3)
+        t_weave(0, 0, 0, "S")
+        v_mult(1)
+        turn(1, 0, 1)
+        v_neg(0)
+        v_neg(1)
+        x_quant(0, 0, 0)
+        v_quant(0, 2)
+        turn(1, 0, 0)
         t_quant(0, 0, 1)
-        x_quant(1, 1, 0)
-        turn(1, 1, 3, "V")
-        t_quant(1, 1, 0)
+        turn(1, 0, 2)
+        v_quant(1, 2)
+        x_quant(1, 0, 0)
+        x_quant(0, 0, 1)
+        v_quant(1, 0)
+        turn(1, 0, 3)
+        x_quant(1, 0, 1)
+        t_quant(0, 0, 0)
+        t_weave(1, 0, 0, "H")
         turn(0, 1, 0)
-        x_quant(1, 1, 1)
-        squares(0, 0, 1)
+        t_weave(1, 1, 0, "S")
+        warm(9)
+        warm(10)
+        warm(11)
+        warm(12)
+        turn(1, 1, 1, "V")
+        stage1(0, 0, 0)
+        t_weave(1, 0, 1, "V")
+        squares(0, 0, 0)
+        turn(1, 1, 0)
+        t_quant(1, 1, 0)
+        turn(1, 1, 2)
+        t_quant(1, 0, 0)
+        turn(0, 1, 2)
+        stage1(0, 0, 1)
+        turn(0, 1, 1)
+        turn(1, 1, 3)
+        t_quant(1, 0, 1)
+        x_quant(1, 1, 0)
+        dev1(0, 0)
         x_quant(0, 1, 0)
-        dev2(0, 0)
+        x_quant(1, 1, 1)
+        turn(0, 1, 3)
+        x_quant(0, 1, 1)
         stage1(0, 1, 0)
+        squares(0, 0, 1)
+        dev2(0, 0)
         stage1(0, 1, 1)
         squares(0, 1, 0)
-        stage1(1, 0, 0)
         dev1(0, 1)
-        stage1(1, 0, 1)
         squares(0, 1, 1)
-        stage1(1, 1, 0)
-        squares(1, 0, 0)
-        squares(1, 0, 1)
         err(0, 0, 1)
+        r_scaled(1)
         dev2(0, 1)
-        squares(1, 1, 0)
+        stage1(1, 0, 0)
+        stage1(1, 0, 1)
         err(0, 0, 0)
-        stage1(1, 1, 1)
+        squares(1, 0, 0)
+        err(0, 1, 1)
+        squares(1, 0, 1)
+        stage1(1, 1, 0)
         err(0, 1, 0)
         dev1(1, 0)
+        stage1(1, 1, 1)
+        squares(1, 1, 0)
         err_neg(0, 2)
-        dev2(1, 0)
         squares(1, 1, 1)
-        err(0, 1, 1)
-        err(1, 0, 0)
+        dev2(1, 0)
         dev1(1, 1)
-        err_quant(0, 2)
-        dev2(1, 1)
-        t_weave(0, 1, 0, "S")
-        err_neg(1, 0)
+        err(1, 0, 0)
         err(1, 0, 1)
-        err(1, 1, 0)
-        stage2(0, 0, 0)
-        t_weave(0, 1, 1, "S")
-        err_quant(1, 0)
+        dev2(1, 1)
+        err_quant(0, 2)
         stage2(0, 3, 0)
+        stage2(0, 0, 0)
         err(1, 1, 1)
-        err_neg(1, 1)
-        t_quant(0, 1, 0)
         stage2(0, 2, 0)
+        err_neg(1, 0)
+        t_weave(0, 1, 0, "S")
+        err(1, 1, 0)
+        t_quant(0, 1, 0)
+        err_neg(1, 1)
+        err_quant(1, 0)
         err_quant(1, 1)
         t_weave(1, 1, 1, "H")
         stage2(0, 1, 0)
-        t_quant(0, 1, 1)
-        stage2(0, 1, 1)
-        stage2(0, 3, 1)
+        t_weave(0, 1, 1, "S")
         stage2(0, 0, 1)
-        stage2(0, 2, 1)
-        leave(0, 1, 2)
-        t_quant(1, 0, 1)
         t_quant(1, 1, 1)
+        t_quant(0, 1, 1)
+        leave(0, 0, 2)
+        stage2(0, 2, 1)
+        stage2(0, 1, 1)
+        leave(0, 1, 2, "V")
+        stage2(0, 3, 1)
+        stage2h(1, 2, 0)
+        leave(0, 3, 2, "V")
+        stage2h(1, 3, 0)
+        leave(1, 3, 0, "V")
         stage2h(1, 0, 0)
         stage2h(1, 1, 0)
-        stage2h(1, 1, 1)
-        stage2h(1, 3, 0)
-        leave(0, 0, 2)
-        leave(0, 3, 2)
-        leave(0, 2, 2, "V")
+        stage2h(1, 0, 1)
+        leave(0, 2, 2)
         store_out(0, 0)
         store_out(0, 1)
-        stage2h(1, 2, 0)
         stage2h(1, 3, 1)
+        leave(1, 1, 0)
+        stage2h(1, 1, 1)
+        leave(1, 0, 0)
         out_weave(0, 2)
+        leave(1, 3, 1)
+        leave(1, 0, 1)
+        leave(1, 1, 1)
+        stage2h(1, 2, 1)
+        leave(1, 2, 0, "V")
+        store_out(1, 0)
+        out_weave(1, 0)
         out_quant(0, 2)
         store_words(0, 0, 2)
         store_scales(0)
-        stage2h(1, 0, 1)
-        leave(1, 3, 0, "V")
-        leave(1, 1, 0)
-        leave(1, 0, 0)
-        leave(1, 2, 0)
-        store_out(1, 0)
-        leave(1, 1, 1)
-        out_weave(1, 0)
-        leave(1, 3, 1)
         out_quant(1, 0)
         store_words(1, 0, 1)
-        stage2h(1, 2, 1)
-        leave(1, 0, 1)
         leave(1, 2, 1)
         store_out(1, 1)
         out_weave(1, 1)

@@ -84,7 +84,6 @@ def tile_godardconstantmodulusgradient_x1_kernel(tc, y, w, q, a, r, out, words, 
         k_col = kt("k_col", [P, 8], F32)
         s_col = kt("s_col", [P, 8], F32)
         a_col = kt("a_col", [P, 8], F32)
-        rr = kt("rr", [P, 2, 2, 4, P], F32)
         q_flat = q_bf[:].rearrange("p g j -> p (g j)")
         nc.scalar.copy(out=r_f[:], in_=r_bf[:])
         nc.scalar.activation(out=k_col[:], in_=q_flat, func=ACT.Square, scale=2.0**-2.5)
@@ -96,15 +95,6 @@ def tile_godardconstantmodulusgradient_x1_kernel(tc, y, w, q, a, r, out, words, 
             for u in (0, 1):
                 nc.tensor.transpose(rp[:, u, :], r_f[:, u : u + 1].to_broadcast([P, P]), ident[:])
             nc.scalar.copy(out=r_b[:].rearrange("p (n u) -> p n u", u=2), in_=rp[:].rearrange("p u n -> p n u"))
-
-        def r_scaled(g):
-            for j in range(4):
-                nc.scalar.activation(
-                    out=rr[:, g, :, j, :],
-                    in_=r_b[:].rearrange("p (h n) -> p h n", h=2),
-                    func=ACT.Copy,
-                    scale=k_col[:, 4 * g + j : 4 * g + j + 1],
-                )
 
         v_bf, v_codes, v_scales = {}, {}, {}
         for G in (0, 1):
@@ -242,16 +232,24 @@ def tile_godardconstantmodulusgradient_x1_kernel(tc, y, w, q, a, r, out, words, 
         def dev1(g, h):
             u = stage.tile([P, 4, P], F32, name="u", align_bytes=64, bufs=2)
             dev[g, h, 0] = u
-            nc.vector.tensor_tensor(out=u[:], in0=sq[g, h][:, 0], in1=rr[:, g, h], op=ALU.subtract)
+            for j in range(4):
+                nc.vector.scalar_tensor_tensor(
+                    out=u[:, j, :],
+                    in0=r_b[:, 128 * h : 128 * h + 128],
+                    scalar=k_col[:, 4 * g + j : 4 * g + j + 1],
+                    in1=sq[g, h][:, 0, j, :],
+                    op0=ALU.mult,
+                    op1=ALU.subtract,
+                )
 
         def dev2(g, h):
             m = stage.tile([P, P, 4], F32, name="m", align_bytes=64, bufs=2)
             dev[g, h, 1] = m
             nc.vector.tensor_tensor(
                 out=m[:],
-                in0=dev[g, h, 0][:].rearrange("p j n -> p n j"),
-                in1=sq[g, h][:, 1].rearrange("p j n -> p n j"),
-                op=ALU.add,
+                in0=sq[g, h][:, 1].rearrange("p j n -> p n j"),
+                in1=dev[g, h, 0][:].rearrange("p j n -> p n j"),
+                op=ALU.subtract,
             )
 
         def err(g, h, x):
@@ -381,136 +379,134 @@ def tile_godardconstantmodulusgradient_x1_kernel(tc, y, w, q, a, r, out, words, 
         warm(6)
         warm(7)
         warm(8)
-        r_scaled(0)
         turn(0, 0, 0)
-        turn(0, 0, 1)
-        turn(0, 0, 2)
         v_mult(0)
-        v_quant(0, 0)
-        t_weave(0, 0, 1, "V")
+        turn(0, 0, 1)
         turn(0, 0, 3)
-        t_weave(0, 0, 0, "S")
-        v_mult(1)
-        turn(1, 0, 1)
+        v_quant(0, 0)
         v_neg(0)
-        v_neg(1)
-        x_quant(0, 0, 0)
-        v_quant(0, 2)
-        turn(1, 0, 0)
+        turn(0, 0, 2)
+        t_weave(0, 0, 0, "S")
+        t_weave(0, 0, 1, "V")
+        v_mult(1)
+        turn(1, 0, 1, "V")
         t_quant(0, 0, 1)
-        turn(1, 0, 2)
-        v_quant(1, 2)
-        x_quant(1, 0, 0)
-        x_quant(0, 0, 1)
+        turn(1, 0, 0)
         v_quant(1, 0)
+        x_quant(0, 0, 0)
+        v_neg(1, "S")
         turn(1, 0, 3)
-        x_quant(1, 0, 1)
+        turn(1, 0, 2)
+        x_quant(0, 0, 1)
         t_quant(0, 0, 0)
-        t_weave(1, 0, 0, "H")
-        turn(0, 1, 0)
-        t_weave(1, 1, 0, "S")
+        v_quant(0, 2)
+        turn(0, 1, 3)
+        x_quant(1, 0, 0)
+        t_weave(1, 1, 0, "H")
+        turn(0, 1, 2)
+        x_quant(1, 0, 1)
+        v_quant(1, 2)
         warm(9)
         warm(10)
+        t_weave(1, 0, 0, "V")
+        t_weave(1, 0, 1, "V")
         warm(11)
         warm(12)
-        turn(1, 1, 1, "V")
-        stage1(0, 0, 0)
-        t_weave(1, 0, 1, "V")
-        squares(0, 0, 0)
-        turn(1, 1, 0)
-        t_quant(1, 1, 0)
         turn(1, 1, 2)
         t_quant(1, 0, 0)
-        turn(0, 1, 2)
-        stage1(0, 0, 1)
-        turn(0, 1, 1)
-        turn(1, 1, 3)
-        t_quant(1, 0, 1)
-        x_quant(1, 1, 0)
-        dev1(0, 0)
-        x_quant(0, 1, 0)
-        x_quant(1, 1, 1)
-        turn(0, 1, 3)
+        stage1(0, 0, 0)
+        squares(0, 0, 0)
         x_quant(0, 1, 1)
-        stage1(0, 1, 0)
+        turn(0, 1, 1)
+        dev1(0, 0)
+        turn(1, 1, 3)
+        turn(0, 1, 0)
+        stage1(0, 0, 1)
         squares(0, 0, 1)
+        turn(1, 1, 0)
+        t_quant(1, 0, 1)
+        x_quant(1, 1, 1)
         dev2(0, 0)
+        turn(1, 1, 1)
+        x_quant(0, 1, 0)
+        stage1(0, 1, 0)
+        x_quant(1, 1, 0)
         stage1(0, 1, 1)
-        squares(0, 1, 0)
-        dev1(0, 1)
-        squares(0, 1, 1)
-        err(0, 0, 1)
-        r_scaled(1)
-        dev2(0, 1)
-        stage1(1, 0, 0)
-        stage1(1, 0, 1)
         err(0, 0, 0)
-        squares(1, 0, 0)
-        err(0, 1, 1)
-        squares(1, 0, 1)
+        squares(0, 1, 0)
+        err(0, 0, 1)
         stage1(1, 1, 0)
-        err(0, 1, 0)
-        dev1(1, 0)
+        dev1(0, 1)
+        stage1(1, 0, 0)
+        t_quant(1, 1, 0)
         stage1(1, 1, 1)
+        squares(0, 1, 1)
+        dev2(0, 1)
+        t_weave(1, 1, 1, "H")
+        err(0, 1, 1)
+        err(0, 1, 0)
+        squares(1, 0, 0)
         squares(1, 1, 0)
-        err_neg(0, 2)
+        stage1(1, 0, 1)
         squares(1, 1, 1)
-        dev2(1, 0)
+        dev1(1, 0)
+        squares(1, 0, 1)
         dev1(1, 1)
-        err(1, 0, 0)
-        err(1, 0, 1)
+        err_neg(0, 2)
         dev2(1, 1)
-        err_quant(0, 2)
-        stage2(0, 3, 0)
-        stage2(0, 0, 0)
+        dev2(1, 0)
+        err(1, 1, 0)
         err(1, 1, 1)
+        err_quant(0, 2)
+        stage2(0, 1, 0)
+        err_neg(1, 1)
+        stage2(0, 0, 0)
+        err(1, 0, 0)
+        err_quant(1, 1)
+        t_weave(0, 1, 0, "S")
+        stage2(0, 3, 0)
+        err(1, 0, 1)
         stage2(0, 2, 0)
         err_neg(1, 0)
-        t_weave(0, 1, 0, "S")
-        err(1, 1, 0)
         t_quant(0, 1, 0)
-        err_neg(1, 1)
         err_quant(1, 0)
-        err_quant(1, 1)
-        t_weave(1, 1, 1, "H")
-        stage2(0, 1, 0)
-        t_weave(0, 1, 1, "S")
-        stage2(0, 0, 1)
+        stage2(0, 1, 1)
+        t_weave(0, 1, 1, "H")
+        stage2(0, 3, 1)
+        leave(0, 1, 2)
+        stage2(0, 2, 1)
         t_quant(1, 1, 1)
+        stage2(0, 0, 1)
         t_quant(0, 1, 1)
         leave(0, 0, 2)
-        stage2(0, 2, 1)
-        stage2(0, 1, 1)
-        leave(0, 1, 2, "V")
-        stage2(0, 3, 1)
         stage2h(1, 2, 0)
-        leave(0, 3, 2, "V")
-        stage2h(1, 3, 0)
-        leave(1, 3, 0, "V")
         stage2h(1, 0, 0)
+        leave(1, 2, 0)
+        stage2h(1, 3, 0)
+        leave(1, 0, 0)
         stage2h(1, 1, 0)
-        stage2h(1, 0, 1)
-        leave(0, 2, 2)
+        leave(0, 2, 2, "V")
+        leave(0, 3, 2, "V")
         store_out(0, 0)
         store_out(0, 1)
-        stage2h(1, 3, 1)
+        leave(1, 3, 0)
         leave(1, 1, 0)
-        stage2h(1, 1, 1)
-        leave(1, 0, 0)
-        out_weave(0, 2)
-        leave(1, 3, 1)
-        leave(1, 0, 1)
-        leave(1, 1, 1)
-        stage2h(1, 2, 1)
-        leave(1, 2, 0, "V")
         store_out(1, 0)
-        out_weave(1, 0)
+        stage2h(1, 1, 1)
+        out_weave(0, 2)
+        stage2h(1, 0, 1)
         out_quant(0, 2)
         store_words(0, 0, 2)
         store_scales(0)
+        leave(1, 1, 1)
+        stage2h(1, 2, 1)
+        leave(1, 0, 1, "V")
+        stage2h(1, 3, 1)
+        out_weave(1, 0)
+        leave(1, 2, 1)
         out_quant(1, 0)
         store_words(1, 0, 1)
-        leave(1, 2, 1)
+        leave(1, 3, 1)
         store_out(1, 1)
         out_weave(1, 1)
         out_quant(1, 1)

from contextlib import ExitStack

import concourse.mybir as mybir
from concourse.masks import make_identity

F32 = mybir.dt.float32
BF16 = mybir.dt.bfloat16
U32 = mybir.dt.uint32
I32 = mybir.dt.int32
U8 = mybir.dt.uint8
FP8X4 = mybir.dt.float8_e4m3fn_x4
ACT = mybir.ActivationFunctionType
ALU = mybir.AluOpType

P = 128
C, T, D, J = 2, 1024, 1024, 256
FLOPS = 8 * 2 * T * D * J


def tile_godardconstantmodulusgradient_x1_kernel(tc, y, w, q, a, r, out, words, scales):
    nc = tc.nc
    with ExitStack() as ctx:
        keep = ctx.enter_context(tc.tile_pool(name="keep", bufs=1))
        stage = ctx.enter_context(tc.tile_pool(name="stage", bufs=4))
        psum = ctx.enter_context(tc.psum_pool(name="psum", bufs=1))
        ctx.enter_context(tc.manual_schedule())

        def kt(name, shape, dt):
            return keep.tile(shape, dt, name=name, align_bytes=64)

        a_bf = kt("a_bf", [P, 2, 4], BF16)
        q_bf = kt("q_bf", [P, 2, 4], BF16)
        r_bf = kt("r_bf", [P, 2], BF16)
        nc.scalar.dma_start(out=a_bf[:], in_=a.rearrange("(g p j) -> p g j", p=P, j=4))
        nc.scalar.dma_start(out=q_bf[:], in_=q.rearrange("(g p j) -> p g j", p=P, j=4))
        nc.scalar.dma_start(out=r_bf[:], in_=r.rearrange("(p u) -> p u", u=2))
        w_raw = {G: keep.tile([P, 2, 4, J], BF16, name="w_raw%d" % G, tag="wo%d" % G, align_bytes=64) for G in (0, 1)}
        y_raw = {(c, g): kt("y_raw%d%d" % (c, g), [P, 4, D], BF16) for c in (0, 1) for g in (0, 1)}

        def load_w(G, c):
            nc.sync.dma_start(
                out=w_raw[G][:, c],
                in_=w[c, 512 * G : 512 * G + 512, :].rearrange("(p j) n -> p j n", j=4),
            )

        def load_y(c, g):
            src = y[c, 512 * g : 512 * g + 512, :].rearrange("(p j) d -> p j d", j=4)
            for j0 in (0, 2):
                nc.sync.dma_start(out=y_raw[c, g][:, j0 : j0 + 2], in_=src[:, j0 : j0 + 2])

        load_w(0, 0)
        load_w(0, 1)
        load_y(0, 0)
        load_w(1, 0)
        load_w(1, 1)
        load_y(1, 0)
        load_y(0, 1)
        load_y(1, 1)

        ident = kt("ident", [P, P], F32)
        make_identity(nc, ident[:])

        w1_bf = stage.tile([P, 2, 4, P, 4], BF16, name="ti", align_bytes=64, bufs=4)
        w1_codes = kt("w1_codes", [P, 256], U32)
        w1_scales = kt("w1_scales", [P, 256], U8)
        w1_in = w1_bf[:, 0, 0:2].rearrange("p t m j -> p (t m j)")
        nc.vector.memset(w1_in, 0.0)
        nc.vector.quantize_mx(out=w1_codes[:].bitcast(FP8X4), scales=w1_scales[:], in_=w1_in)

        def warm(i):
            wt = psum.tile([P, 256], F32, name="wt", tag="b7")
            nc.tensor.matmul_mx(
                out=wt[:],
                lhsT=w1_codes[:, 0:128].bitcast(FP8X4),
                lhsT_scale=w1_scales[:, 0:128],
                rhs=w1_codes[:].bitcast(FP8X4),
                rhs_scale=w1_scales[:],
                start=True,
                stop=True,
            )

        r_f = kt("r_f", [P, 2], F32)
        r_b = kt("r_b", [P, J], F32)
        k_col = kt("k_col", [P, 8], F32)
        s_col = kt("s_col", [P, 8], F32)
        a_col = kt("a_col", [P, 8], F32)
        q_flat = q_bf[:].rearrange("p g j -> p (g j)")
        nc.scalar.copy(out=r_f[:], in_=r_bf[:])
        nc.scalar.activation(out=k_col[:], in_=q_flat, func=ACT.Square, scale=2.0**-2.5)
        nc.scalar.activation(out=s_col[:], in_=q_flat, func=ACT.Square, scale=2.0**-1.25)
        nc.scalar.copy(out=a_col[:], in_=a_bf[:].rearrange("p g j -> p (g j)"))

        def r_bcast():
            rp = psum.tile([P, 2, P], F32, name="rp", tag="b0")
            for u in (0, 1):
                nc.tensor.transpose(rp[:, u, :], r_f[:, u : u + 1].to_broadcast([P, P]), ident[:])
            nc.scalar.copy(out=r_b[:].rearrange("p (n u) -> p n u", u=2), in_=rp[:].rearrange("p u n -> p n u"))

        v_bf, v_codes, v_scales = {}, {}, {}
        for G in (0, 1):
            v_bf[G] = kt("v_bf%d" % G, [P, 3, J, 4], BF16)
            v_codes[G] = kt("v_codes%d" % G, [P, 3 * J], U32)
            v_scales[G] = kt("v_scales%d" % G, [P, 3 * J], U8)

        def v_mult(G):
            for cs in ((slice(0, 1), slice(1, 2)) if G == 0 else (slice(0, 2),)):
                n = cs.stop - cs.start
                nc.vector.tensor_tensor(
                    out=v_bf[G][:, cs],
                    in0=w_raw[G][:, cs].rearrange("p c j n -> p c n j"),
                    in1=a_bf[:, G, :].unsqueeze(1).unsqueeze(1).to_broadcast([P, n, J, 4]),
                    op=ALU.mult,
                )

        def v_neg(G, eng="V"):
            vi = v_bf[G][:, 1].rearrange("p n j -> p (n j)")
            vn = v_bf[G][:, 2].rearrange("p n j -> p (n j)")
            if eng == "S":
                nc.scalar.activation(out=vn, in_=vi, func=ACT.Copy, scale=-1.0)
            else:
                nc.vector.tensor_scalar(out=vn, in0=vi, scalar1=-1.0, scalar2=None, op0=ALU.mult)

        def v_quant(G, lo):
            n = 2 if lo == 0 else 1
            nc.vector.quantize_mx(
                out=v_codes[G][:, lo * J : (lo + n) * J].bitcast(FP8X4),
                scales=v_scales[G][:, lo * J : (lo + n) * J],
                in_=v_bf[G][:, lo : lo + n].rearrange("p s n j -> p (s n j)"),
            )

        x_codes, x_scales, yt = {}, {}, {}
        for c in (0, 1):
            for g in (0, 1):
                x_codes[c, g] = kt("x_codes%d%d" % (c, g), [P, 4, 2, P], U32)
                x_scales[c, g] = kt("x_scales%d%d" % (c, g), [P, 4, 2, P], U8)

        turns = []

        def turn(c, g, j, eng="S"):
            if (c, g, j // 2) not in yt:
                yt[c, g, j // 2] = stage.tile([P, 2, 2, P, 2], F32, name="yt", align_bytes=64)
            tp = psum.tile([P, 2, 2, P], F32, name="tp", tag="b%d" % (len(turns) % 4))
            turns.append(j)
            wordsv = y_raw[c, g][:, j, :].bitcast(F32)
            for G in (0, 1):
                for u in (0, 1):
                    nc.tensor.transpose(tp[:, G, u, :], wordsv[:, 256 * G + u : 256 * (G + 1) : 2], ident[:])
            dst, src = yt[c, g, j // 2][:, j % 2], tp[:].rearrange("p g u r -> p g r u")
            if eng == "S":
                nc.scalar.copy(out=dst, in_=src)
            else:
                nc.vector.tensor_copy(out=dst, in_=src)

        def x_quant(c, g, h):
            nc.vector.quantize_mx(
                out=x_codes[c, g][:, 2 * h : 2 * h + 2].rearrange("p j g r -> p (j g r)").bitcast(FP8X4),
                scales=x_scales[c, g][:, 2 * h : 2 * h + 2].rearrange("p j g r -> p (j g r)"),
                in_=yt[c, g, h][:].rearrange("p j g r u -> p (j g r u)").bitcast(BF16),
            )

        t_codes, t_scales, ti = {}, {}, {}
        for c in (0, 1):
            for g in (0, 1):
                t_codes[c, g] = kt("t_codes%d%d" % (c, g), [P, D], U32)
                t_scales[c, g] = kt("t_scales%d%d" % (c, g), [P, D], U8)

        def weave_part(c, g, G, m0, n, eng):
            dst = ti[c, g][:, G, :, m0 : m0 + n, :].rearrange("p t m j -> p m j t")
            src = y_raw[c, g][:, :, 512 * G + 4 * m0 : 512 * G + 4 * (m0 + n)].rearrange("p j (m t) -> p m j t", t=4)
            if eng == "S":
                nc.scalar.copy(out=dst, in_=src)
            else:
                nc.vector.tensor_copy(out=dst, in_=src)

        def t_weave(c, g, G, eng):
            if (c, g) not in ti:
                ti[c, g] = stage.tile([P, 2, 4, P, 4], BF16, name="ti", align_bytes=64, bufs=4)
            if eng == "V":
                weave_part(c, g, G, 0, 128, "V")
            else:
                weave_part(c, g, G, 0, 64, "S" if eng == "S" else "V")
                weave_part(c, g, G, 64, 64, "S")

        def t_quant(c, g, G):
            lo, n = (0, D) if G == 2 else (512 * G, 512)
            nc.vector.quantize_mx(
                out=t_codes[c, g][:, lo : lo + n].bitcast(FP8X4),
                scales=t_scales[c, g][:, lo : lo + n],
                in_=ti[c, g][:].rearrange("p g t m j -> p (g t m j)")[:, 4 * lo : 4 * (lo + n)],
            )

        z = {}
        sq, dev = {}, {}
        e_bf, e_codes, e_scales = {}, {}, {}
        for g in (0, 1):
            e_bf[g] = kt("e_bf%d" % g, [P, 3, J, 4], BF16)
            e_codes[g] = kt("e_codes%d" % g, [P, 3 * J], U32)
            e_scales[g] = kt("e_scales%d" % g, [P, 3 * J], U8)

        def stage1(g, h, x):
            b = (4 if g == 0 else 0) + 2 * h + x
            zt = psum.tile([P, 4, P], F32, name="z", tag="b%d" % b)
            z[g, h, x] = zt
            slots = (0, 2) if x == 0 else (1, 0)
            for j in range(4):
                n = 0
                for c in (0, 1):
                    lo = slots[c] * J + 128 * h
                    for G in (0, 1):
                        nc.tensor.matmul_mx(
                            out=zt[:, j, :],
                            lhsT=x_codes[c, g][:, j, G, :].bitcast(FP8X4),
                            lhsT_scale=x_scales[c, g][:, j, G, :],
                            rhs=v_codes[G][:, lo : lo + 128].bitcast(FP8X4),
                            rhs_scale=v_scales[G][:, lo : lo + 128],
                            start=(n == 0),
                            stop=(n == 3),
                        )
                        n += 1

        def squares(g, h, x):
            if (g, h) not in sq:
                sq[g, h] = stage.tile([P, 2, 4, P], F32, name="sq", align_bytes=64, bufs=2)
            for j in range(4):
                nc.scalar.activation(
                    out=sq[g, h][:, x, j, :],
                    in_=z[g, h, x][:, j, :],
                    func=ACT.Square,
                    scale=s_col[:, 4 * g + j : 4 * g + j + 1],
                )

        def dev1(g, h):
            u = stage.tile([P, 4, P], F32, name="u", align_bytes=64, bufs=2)
            dev[g, h, 0] = u
            for j in range(4):
                nc.vector.scalar_tensor_tensor(
                    out=u[:, j, :],
                    in0=r_b[:, 128 * h : 128 * h + 128],
                    scalar=k_col[:, 4 * g + j : 4 * g + j + 1],
                    in1=sq[g, h][:, 0, j, :],
                    op0=ALU.mult,
                    op1=ALU.subtract,
                )

        def dev2(g, h):
            m = stage.tile([P, P, 4], F32, name="m", align_bytes=64, bufs=2)
            dev[g, h, 1] = m
            nc.vector.tensor_tensor(
                out=m[:],
                in0=sq[g, h][:, 1].rearrange("p j n -> p n j"),
                in1=dev[g, h, 0][:].rearrange("p j n -> p n j"),
                op=ALU.subtract,
            )

        def err(g, h, x):
            nc.vector.tensor_tensor(
                out=e_bf[g][:, x, 128 * h : 128 * h + 128, :],
                in0=z[g, h, x][:].rearrange("p j n -> p n j"),
                in1=dev[g, h, 1][:],
                op=ALU.mult,
            )

        def err_neg(g, h):
            lo, n = (0, J) if h == 2 else (128 * h, 128)
            nc.vector.tensor_scalar(
                out=e_bf[g][:, 2, lo : lo + n, :].rearrange("p n j -> p (n j)"),
                in0=e_bf[g][:, 0, lo : lo + n, :].rearrange("p n j -> p (n j)"),
                scalar1=-1.0,
                scalar2=None,
                op0=ALU.mult,
            )

        def quant_err(g, lo, n):
            nc.vector.quantize_mx(
                out=e_codes[g][:, lo : lo + n].bitcast(FP8X4),
                scales=e_scales[g][:, lo : lo + n],
                in_=e_bf[g][:].rearrange("p x n j -> p (x n j)")[:, 4 * lo : 4 * (lo + n)],
            )

        def err_quant(g, h):
            if h == 2:
                quant_err(g, 0, 2 * J)
                quant_err(g, 2 * J, J)
            else:
                for x in (0, 1, 2):
                    quant_err(g, x * J + 128 * h, 128)

        acc, res, ob, o_codes, o_scales = {}, {}, {}, {}, {}
        for G in (0, 1):
            res[G] = kt("res%d" % G, [P, 2, 4, J], F32)
            o_codes[G] = kt("o_codes%d" % G, [P, 2 * J], U32)
            o_scales[G] = kt("o_scales%d" % G, [P, 2 * J], U8)

        def stage2(G, t, g):
            if g == 0:
                acc[G, t] = psum.tile([P, 2 * J], F32, name="acc", tag="b%d" % ((4 if G == 0 else 0) + t))
            lo = 512 * G + 128 * t
            for c in (0, 1):
                nc.tensor.matmul_mx(
                    out=acc[G, t][:],
                    lhsT=t_codes[c, g][:, lo : lo + 128].bitcast(FP8X4),
                    lhsT_scale=t_scales[c, g][:, lo : lo + 128],
                    rhs=e_codes[g][:, c * J : c * J + 512].bitcast(FP8X4),
                    rhs_scale=e_scales[g][:, c * J : c * J + 512],
                    start=(g == 0 and c == 0),
                    stop=(g == 1 and c == 1),
                )

        def stage2h(G, t, c):
            if c == 0:
                acc[G, t] = psum.tile([P, 2 * J], F32, name="acc", tag="b%d" % ((4 if G == 0 else 0) + t))
            lo = 512 * G + 128 * t
            for g in (0, 1):
                for part in (0, 1):
                    nc.tensor.matmul_mx(
                        out=acc[G, t][:, c * J : (c + 1) * J],
                        lhsT=t_codes[part, g][:, lo : lo + 128].bitcast(FP8X4),
                        lhsT_scale=t_scales[part, g][:, lo : lo + 128],
                        rhs=e_codes[g][:, (c + part) * J : (c + part + 1) * J].bitcast(FP8X4),
                        rhs_scale=e_scales[g][:, (c + part) * J : (c + part + 1) * J],
                        start=(g == 0 and part == 0),
                        stop=(g == 1 and part == 1),
                    )

        def leave(G, t, c, eng="S"):
            if c == 2:
                dst, src = res[G][:, :, t, :], acc[G, t][:].rearrange("p (c n) -> p c n", c=2)
            else:
                dst, src = res[G][:, c, t, :], acc[G, t][:, c * J : (c + 1) * J]
            gain = a_col[:, 4 * G + t : 4 * G + t + 1]
            if eng == "S":
                nc.scalar.activation(out=dst, in_=src, func=ACT.Copy, scale=gain)
            else:
                nc.vector.tensor_scalar(out=dst, in0=src, scalar1=gain, scalar2=None, op0=ALU.mult)

        def out_weave(G, c):
            if G not in ob:
                ob[G] = keep.tile([P, 2 * J, 4], BF16, name="ob%d" % G, tag="wo%d" % G, align_bytes=64)
            cs = slice(0, 2) if c == 2 else slice(c, c + 1)
            nc.vector.tensor_copy(
                out=ob[G][:].rearrange("p (c n) t -> p c n t", c=2)[:, cs],
                in_=res[G][:, cs].rearrange("p c t n -> p c n t"),
            )

        def out_quant(G, c):
            lo, n = (0, 2 * J) if c == 2 else (c * J, J)
            nc.vector.quantize_mx(
                out=o_codes[G][:, lo : lo + n].bitcast(FP8X4),
                scales=o_scales[G][:, lo : lo + n],
                in_=ob[G][:, lo : lo + n, :].rearrange("p n t -> p (n t)"),
            )

        def store_out(G, c):
            nc.sync.dma_start(
                out=out[c, 512 * G : 512 * G + 512, :].rearrange("(p t) n -> p t n", t=4), in_=res[G][:, c]
            )

        def store_words(G, lo, n):
            nc.sync.dma_start(
                out=words[G].rearrange("p m t -> p (m t)").bitcast(I32)[:, lo * J : (lo + n) * J],
                in_=o_codes[G][:, lo * J : (lo + n) * J].bitcast(I32),
            )

        def store_scales(G):
            for Q in range(4):
                eng = nc.sync if Q % 2 == 0 else nc.scalar
                eng.dma_start(
                    out=scales[G, 4 * Q : 4 * Q + 4, :].bitcast(I32),
                    in_=o_scales[G][32 * Q : 32 * Q + 4, :].bitcast(I32),
                )

        warm(0)
        warm(1)
        warm(2)
        warm(3)
        warm(4)
        r_bcast()
        warm(5)
        warm(6)
        warm(7)
        warm(8)
        turn(0, 0, 0)
        v_mult(0)
        turn(0, 0, 1)
        turn(0, 0, 3)
        v_quant(0, 0)
        v_neg(0)
        turn(0, 0, 2)
        t_weave(0, 0, 0, "S")
        t_weave(0, 0, 1, "V")
        v_mult(1)
        turn(1, 0, 1, "V")
        t_quant(0, 0, 1)
        turn(1, 0, 0)
        v_quant(1, 0)
        x_quant(0, 0, 0)
        v_neg(1, "S")
        turn(1, 0, 3)
        turn(1, 0, 2)
        x_quant(0, 0, 1)
        t_quant(0, 0, 0)
        v_quant(0, 2)
        turn(0, 1, 3)
        x_quant(1, 0, 0)
        t_weave(1, 1, 0, "H")
        turn(0, 1, 2)
        x_quant(1, 0, 1)
        v_quant(1, 2)
        warm(9)
        warm(10)
        t_weave(1, 0, 0, "V")
        t_weave(1, 0, 1, "V")
        warm(11)
        warm(12)
        turn(1, 1, 2)
        t_quant(1, 0, 0)
        stage1(0, 0, 0)
        squares(0, 0, 0)
        x_quant(0, 1, 1)
        turn(0, 1, 1)
        dev1(0, 0)
        turn(1, 1, 3)
        turn(0, 1, 0)
        stage1(0, 0, 1)
        squares(0, 0, 1)
        turn(1, 1, 0)
        t_quant(1, 0, 1)
        x_quant(1, 1, 1)
        dev2(0, 0)
        turn(1, 1, 1)
        x_quant(0, 1, 0)
        stage1(0, 1, 0)
        x_quant(1, 1, 0)
        stage1(0, 1, 1)
        err(0, 0, 0)
        squares(0, 1, 0)
        err(0, 0, 1)
        stage1(1, 1, 0)
        dev1(0, 1)
        stage1(1, 0, 0)
        t_quant(1, 1, 0)
        stage1(1, 1, 1)
        squares(0, 1, 1)
        dev2(0, 1)
        t_weave(1, 1, 1, "H")
        err(0, 1, 1)
        err(0, 1, 0)
        squares(1, 0, 0)
        squares(1, 1, 0)
        stage1(1, 0, 1)
        squares(1, 1, 1)
        dev1(1, 0)
        squares(1, 0, 1)
        dev1(1, 1)
        err_neg(0, 2)
        dev2(1, 1)
        dev2(1, 0)
        err(1, 1, 0)
        err(1, 1, 1)
        err_quant(0, 2)
        stage2(0, 1, 0)
        err_neg(1, 1)
        stage2(0, 0, 0)
        err(1, 0, 0)
        err_quant(1, 1)
        t_weave(0, 1, 0, "S")
        stage2(0, 3, 0)
        err(1, 0, 1)
        stage2(0, 2, 0)
        err_neg(1, 0)
        t_quant(0, 1, 0)
        err_quant(1, 0)
        stage2(0, 1, 1)
        t_weave(0, 1, 1, "H")
        stage2(0, 3, 1)
        leave(0, 1, 2)
        stage2(0, 2, 1)
        t_quant(1, 1, 1)
        stage2(0, 0, 1)
        t_quant(0, 1, 1)
        leave(0, 0, 2)
        stage2h(1, 2, 0)
        stage2h(1, 0, 0)
        leave(1, 2, 0)
        stage2h(1, 3, 0)
        leave(1, 0, 0)
        stage2h(1, 1, 0)
        leave(0, 2, 2, "V")
        leave(0, 3, 2, "V")
        store_out(0, 0)
        store_out(0, 1)
        leave(1, 3, 0)
        leave(1, 1, 0)
        store_out(1, 0)
        stage2h(1, 1, 1)
        out_weave(0, 2)
        stage2h(1, 0, 1)
        out_quant(0, 2)
        store_words(0, 0, 2)
        store_scales(0)
        leave(1, 1, 1)
        stage2h(1, 2, 1)
        leave(1, 0, 1, "V")
        stage2h(1, 3, 1)
        out_weave(1, 0)
        leave(1, 2, 1)
        out_quant(1, 0)
        store_words(1, 0, 1)
        leave(1, 3, 1)
        store_out(1, 1)
        out_weave(1, 1)
        out_quant(1, 1)
        store_words(1, 1, 1)
        store_scales(1)
